import numpy as np, ml_dtypes
CORES = [35,38,43,46]
N = 4
import mx_ref
NC = 256
A = np.float32(0.0125)
BF = ml_dtypes.bfloat16
def cut(t, i, w=512):
    return t[:, w * i:w * i + w]
def tile(rs):
    return np.stack(rs, axis=2).reshape(128, -1).astype(BF)
def setup_inputs(rng):
    def f(*shape):
        return mx_ref.flush((rng.standard_normal(shape, dtype=np.float32) * np.exp2(rng.integers(-2, 3, shape[:-1] + (1,)))).astype(BF))
    return {"q": f(N, 128, 4 * NC), "k": f(N, 128, 4 * 512), "v": f(N, 128, 512)}
def setup_inputs_blocks(rng):
    d = setup_inputs(rng)
    for k in ("v",): d[k] = mx_ref.spread(d[k], rng, 4)
    for k in ("q", "k"): d[k] = mx_ref.spread(d[k], rng, 1)
    return d
def setup_inputs_wide(rng):
    d = setup_inputs(rng)
    for k in ("v",): d[k] = mx_ref.flush((d[k].astype(np.float32) * np.exp2(rng.integers(-8, 9, (N, 1, 1))).astype(np.float32)).astype(BF))
    return d
def setup_inputs_sharp(rng):
    d = setup_inputs(rng); v = d["q"].astype(np.float32).reshape(N, 128, -1, 4)
    d["q"] = mx_ref.flush((v * np.exp2(rng.integers(-2, 4, (N, 1, v.shape[2], 1))).astype(np.float32)).reshape(d["q"].shape).astype(BF))
    return d
def setup_inputs_far(rng):
    d = setup_inputs(rng); d["q"] = (d["q"].astype(np.float32) * 10).astype(BF)
    return d
def setup_inputs_faroff(rng):
    d = setup_inputs(rng); v = d["k"].astype(np.float32).reshape(N, 128, -1, 4)
    d["k"] = mx_ref.flush((v + 192 * rng.standard_normal((1, 128, 1, 4), dtype=np.float32)).reshape(d["k"].shape).astype(BF))
    return d
def reference(q, k, v, own=None):
    ONE = mx_ref.quantize(np.ones((128, 512), BF))
    K = [[mx_ref.quantize(cut(k[j], b)) for b in range(4)] for j in range(N)]; V = [mx_ref.quantize(v[j]) for j in range(N)]
    Q = [mx_ref.quantize(q[i]) for i in range(N)]
    lo = np.zeros((N, N, NC), np.float32); w = lo.copy(); wlo = lo.copy(); whi = lo.copy(); p = np.zeros((N, N, 128, 4 * NC), BF); o = np.zeros((N, 128, NC), np.float32)
    S = [[[mx_ref.matmul(K[j][b], Q[i]) * A for b in range(4)] for i in range(N)] for j in range(N)]
    for j in range(N):
        lo[j] = [np.max(s, axis=(0, 1)) for s in S[j]]
    hi = np.broadcast_to(lo.max(axis=0) + 8, lo.shape).copy()
    c = lo if own is None else own["c"]
    for j in range(N):
        for i in range(N):
            p[j][i] = tile([np.exp(np.maximum(s - c[j][i], -20).astype(np.float64)).astype(np.float32) for s in S[j][i]])
    use = p if own is None else own["p"]
    for i in range(N):
        e = np.exp((c[:, i] - c[:, i].max(axis=0)).astype(np.float64)); wlo[i] = e * (1 - 4e-5); whi[i] = e * (1 + 4e-5)
        w[i] = e if own is None else own["w"][i]
        num = den = 0
        for j in range(N):
            P = mx_ref.quantize(use[j][i])
            num = num + w[i][j].astype(np.float64) * mx_ref.matmul(V[j], P); den = den + w[i][j].astype(np.float64) * mx_ref.matmul(ONE, P)
        o[i] = (num / den).astype(np.float32)
    return {"c": c, "c__lo": lo, "c__hi": hi, "p": p, "w": w, "w__lo": wlo, "w__hi": whi, "o": o}

@@ -1,0 +1,281 @@
+from concourse.bass import DstId, RemoteDMATransfer
+from concourse.mybir import dt, AluOpType, AxisListType, ActivationFunctionType
+
+N = 4
+NC = 256
+A = 0.0125
+RW = 132
+
+SCRATCH = {
+    "qt": ("sbuf", [128, 1024], "bfloat16"),
+    "kt": ("sbuf", [128, 2048], "bfloat16"),
+    "vt": ("sbuf", [128, 512], "bfloat16"),
+    "one": ("sbuf", [128, 512], "bfloat16"),
+    "kc": ("sbuf", [128, 8], "float32"),
+    "ek": ("sbuf", [128, 8], "bfloat16"),
+    "qc": ("sbuf", [128, 1024], "float8_e4m3fn_x4"),
+    "qs": ("sbuf", [128, 1024], "uint8"),
+    "kcd": ("sbuf", [128, 512], "float8_e4m3fn_x4"),
+    "ksc": ("sbuf", [128, 512], "uint8"),
+    "vc": ("sbuf", [128, 256], "float8_e4m3fn_x4"),
+    "vs": ("sbuf", [128, 256], "uint8"),
+    "nm": ("sbuf", [128, 8], "float32"),
+    "nb": ("sbuf", [128, 8], "float32"),
+    "nbl": ("sbuf", [128, 32], "float32"),
+    "mm": ("sbuf", [128, 24], "float32"),
+    "cw": ("sbuf", [128, 32], "float32"),
+    "cwt": ("sbuf", [128, 32], "float32"),
+    "land": ("sbuf", [128, 4 * 2 * RW], "float32"),
+    "acc": ("sbuf", [128, 2 * RW], "float32"),
+    "rd": ("sbuf", [128, 8], "float32"),
+    "on": ("sbuf", [128, 256], "float32"),
+    "ot": ("sbuf", [128, 256], "float32"),
+}
+for _s in range(4):
+    SCRATCH["e%d" % _s] = ("sbuf", [128, 1024], "bfloat16")
+    SCRATCH["i%d" % _s] = ("sbuf", [128, 2, 512], "bfloat16")
+    SCRATCH["x%d" % _s] = ("sbuf", [128, 2, 512], "bfloat16")
+    SCRATCH["p%d" % _s] = ("sbuf", [128, 1024], "bfloat16")
+    SCRATCH["pc%d" % _s] = ("sbuf", [128, 256], "float8_e4m3fn_x4")
+    SCRATCH["ps%d" % _s] = ("sbuf", [128, 256], "uint8")
+    SCRATCH["r%d" % _s] = ("sbuf", [128, 2 * RW], "float32")
+    SCRATCH["tm%d" % _s] = ("sbuf", [128, 2 * RW], "float32")
+for _b in range(8):
+    SCRATCH["bank%d" % _b] = ("psum", [128, 512], "float32")
+
+SEMAPHORES = ["lq", "lk0", "lk1", "lv", "m1", "mk", "mcw", "ek", "qq", "kq0", "kq1", "vq", "oq", "sent", "ca", "cneg", "cown",
+              "mn0", "mn1", "mn2", "wx0", "wx1", "cwt", "sto", "stp", "h1m"]
+for _s in range(4):
+    SEMAPHORES += ["qa%d" % _s, "ra%d" % _s, "tr%d" % _s, "xd%d" % _s, "cl%d" % _s, "qz%d" % _s, "ev%d" % _s, "tm%d" % _s, "ad%d" % _s]
+    for _h in range(2):
+        SEMAPHORES += ["st%d%d" % (_s, _h), "rm%d%d" % (_s, _h), "nb%d%d" % (_s, _h), "ex%d%d" % (_s, _h), "al%d%d" % (_s, _h)]
+for _h in range(2):
+    SEMAPHORES += ["ad3%d" % _h, "tm3%d" % _h, "rc%d" % _h, "nr%d" % _h, "ott%d" % _h]
+
+
+def bits(mask):
+    return [b for b in range(mask.bit_length()) if mask >> b & 1]
+
+
+def to_mask(bs):
+    return sum(1 << b for b in bs)
+
+
+def rank_program(g, core, T, topo):
+    r = T.rank_of(core)
+    if r is None:
+        return
+    S = T.sem
+    F = ActivationFunctionType
+    O = AluOpType
+    V, X, P, Y = g.vector, g.scalar, g.tensor, g.sync
+    others = [i for i in range(N) if i != r]
+    near = [i for i in others if topo.chip(T.cores[i]) == topo.chip(core)][0]
+    far = [i for i in others if i != near]
+    mate = [i for i in far if topo.die(T.cores[i]) == topo.die(core)][0]
+    diag = [i for i in far if i != mate][0]
+    rk = [r, mate, diag, near]
+    addr = {i: topo.addr(T.cores[i]) for i in others}
+    off = bits(topo.mask(core, T.cores[mate]) & topo.mask(core, T.cores[diag]))
+    on = bits(topo.mask(core, T.cores[near]))
+    half = len(off) // 2
+    eng = {mate: off[:half], diag: off[half:], near: [b for b in on if b not in off]}
+    retm = {mate: off, diag: off, near: on}
+    sent = [0]
+
+    def tr(i, src, dst, sem):
+        sent[0] += len(eng[i])
+        return RemoteDMATransfer(dst_ids=[DstId(rid=addr[i][0], pnc=addr[i][1])], dma_engine_mask=to_mask(eng[i]), remote_sem=sem, src=src, dst=dst)
+
+    Y.dma_start(T.qt[:], T.q[:]).then_inc(S.lq, 16)
+    X.dma_start(T.kt[:, 0:1024], T.k[:, 0:1024]).then_inc(S.lk0, 16)
+    Y.dma_start(T.kt[:, 1024:2048], T.k[:, 1024:2048]).then_inc(S.lk1, 16)
+    X.dma_start(T.vt[:], T.v[:]).then_inc(S.lv, 16)
+
+    sl = slice(NC * r, NC * r + NC)
+    g.wait_ge(S.qq, 1)
+    g.remote_dma_fused([tr(i, T.qc[:, sl].bitcast(dt.uint8), T.qc[:, sl].bitcast(dt.uint8), S["qa%d" % r]) for i in (mate, diag, near)], local_sem=S.sent)
+    g.remote_dma_fused([tr(i, T.qs[:, sl], T.qs[:, sl], S["qa%d" % r]) for i in (mate, diag, near)], local_sem=S.sent)
+    for s in range(4):
+        for h in range(2):
+            g.wait_ge(S["nb%d%d" % (s, h)], 1)
+    g.remote_dma_fused([tr(i, T.nb[:], T.nbl[:, 8 * r:8 * r + 8], S.ca) for i in (mate, diag, near)], local_sem=S.sent)
+    for s in (1, 2, 3):
+        i = rk[s]
+        g.wait_ge(S["ev%d" % s], 2)
+        g.remote_dma(T["land"][:, 2 * RW * r:2 * RW * (r + 1)], T["r%d" % s][:], S["ra%d" % r], S.sent, addr[i][1], addr[i][0], to_mask(retm[i]))
+        sent[0] += len(retm[i])
+    g.wait_ge(S.sent, sent[0])
+
+    def scores(s):
+        i = rk[s]
+        if s == 0:
+            P.wait_ge(S.qq, 1)
+            P.wait_ge(S.kq0, 1)
+            P.wait_ge(S.kq1, 1)
+        else:
+            P.wait_ge(S["qa%d" % i], 2 * len(eng[i]))
+        for h in range(2):
+            c0 = NC * i + 128 * h
+            P.matmul_mx(T["bank%d" % (2 * s + h)][:], T.qc[:, c0:c0 + 128], T.qs[:, c0:c0 + 128], T.kcd[:], T.ksc[:], True, True).then_inc(S["st%d%d" % (s, h)], 1)
+
+    albank = {1: 0, 2: 2, 0: 4, 3: 6}
+
+    def values(s):
+        b = albank[s]
+        P.wait_ge(S["qz%d" % s], 1)
+        for h in range(2):
+            P.wait_ge(S["ex%d%d" % (b // 2, h)], 1)
+            P.matmul_mx(T["bank%d" % (b + h)][:, 0:256], T["pc%d" % s][:, 128 * h:128 * h + 128], T["ps%d" % s][:, 128 * h:128 * h + 128],
+                        T.vc[:], T.vs[:], True, True).then_inc(S["al%d%d" % (s, h)], 1)
+
+    for s in range(4):
+        scores(s)
+    P.wait_ge(S.vq, 1)
+    P.wait_ge(S.oq, 1)
+    for s in (1, 2, 0, 3):
+        values(s)
+
+    X.wait_ge(S.mk, 1)
+    X.activation(T.ek[:, 0:1], T.kc[:, 0:1], F.Exp).then_inc(S.ek, 1)
+    for s in range(4):
+        for h in range(2):
+            col = 4 * h + rk[s]
+            X.wait_ge(S["nb%d%d" % (s, h)], 1)
+            X.activation(T["e%d" % s][:, 512 * h:512 * h + 512], T["bank%d" % (2 * s + h)][:], F.Exp, bias=T.nb[:, col:col + 1], scale=A).then_inc(S["ex%d%d" % (s, h)], 1)
+
+    def exchange(q, s, pairs):
+        q.wait_ge(S["tr%d" % s], 8)
+        for kq, tq in pairs:
+            q.dma_start(T["x%d" % s][32 * kq:32 * kq + 32, :, 128 * tq:128 * tq + 128],
+                        T["i%d" % s][32 * tq:32 * tq + 32, :, 128 * kq:128 * kq + 128]).then_inc(S["xd%d" % s], 16)
+
+    blocks = [(kq, tq) for kq in range(4) for tq in range(4)]
+    exchange(X, 3, blocks[8:])
+    for s in (1, 2, 3):
+        for h in range(2):
+            X.wait_ge(S["al%d%d" % (s, h)], 1)
+            X.activation(T["r%d" % s][:, RW * h:RW * h + RW], T["bank%d" % (albank[s] + h)][:, 0:RW], F.Copy).then_inc(S["ev%d" % s], 1)
+    wcol = lambda j, h: T.cw[:, 8 + 4 * h + j:9 + 4 * h + j]
+    X.wait_ge(S.mn2, 1)
+    X.wait_ge(S.cown, 1)
+    X.wait_ge(S.mcw, 1)
+    for h in range(2):
+        X.activation(T.cw[:, 8 + 4 * h:12 + 4 * h], T.nbl[:, 4 * h + r:32:8], F.Exp, bias=T.mm[:, 16 + h:17 + h], scale=-1.0).then_inc(S["wx%d" % h], 1)
+    for h in range(2):
+        X.wait_ge(S["wx%d" % h], 1)
+        X.wait_ge(S["al0%d" % h], 1)
+        X.activation(T.acc[:, RW * h:RW * h + RW], T["bank%d" % (albank[0] + h)][:, 0:RW], F.Copy, scale=wcol(r, h)).then_inc(S.ev0, 1)
+
+    def land(j, h):
+        return T["land"][:, 2 * RW * j + RW * h:2 * RW * j + RW * h + RW]
+
+    for s in (1, 2):
+        X.wait_ge(S["ra%d" % rk[s]], len(retm[rk[s]]))
+        for h in range(2):
+            X.activation(T["tm%d" % s][:, RW * h:RW * h + RW], land(rk[s], h), F.Copy, scale=wcol(rk[s], h)).then_inc(S["tm%d" % s], 1)
+    X.wait_ge(S["ra%d" % near], len(retm[near]))
+    X.activation(T.tm3[:, 0:RW], land(near, 0), F.Copy, scale=wcol(near, 0)).then_inc(S.tm30, 1)
+
+    V.memset(T.one[:], 1.0).then_inc(S.m1, 1)
+    V.memset(T.kc[:], -20.0).then_inc(S.mk, 1)
+    V.memset(T.cw[:], 0.0).then_inc(S.mcw, 1)
+    V.wait_ge(S.m1, 1)
+    V.quantize_mx(T.vc[:, 128:256], T.vs[:, 128:256], T.one[:]).then_inc(S.oq, 1)
+    V.wait_ge(S.lq, 16)
+    V.quantize_mx(T.qc[:, sl], T.qs[:, sl], T.qt[:]).then_inc(S.qq, 1)
+    for n in range(2):
+        V.wait_ge(S["lk%d" % n], 16)
+        V.quantize_mx(T.kcd[:, 256 * n:256 * n + 256], T.ksc[:, 256 * n:256 * n + 256], T.kt[:, 1024 * n:1024 * n + 1024]).then_inc(S["kq%d" % n], 1)
+
+    def shift(s):
+        for h in range(2):
+            col = 4 * h + rk[s]
+            V.wait_ge(S["st%d%d" % (s, h)], 1)
+            V.tensor_reduce(T.nm[:, col:col + 1], T["bank%d" % (2 * s + h)][:], AxisListType.X, O.max, negate=True).then_inc(S["rm%d%d" % (s, h)], 1)
+            V.wait_ge(S["rm%d%d" % (s, h)], 1)
+            V.tensor_scalar(T.nb[:, col:col + 1], T.nm[:, col:col + 1], A, None, O.mult).then_inc(S["nb%d%d" % (s, h)], 1)
+
+    def turn(s):
+        for h in range(2):
+            V.wait_ge(S["ex%d%d" % (s, h)], 1)
+            for b in range(4):
+                V.transpose(T["i%d" % s][:, h, b:512:4], T["e%d" % s][:, 512 * h + 128 * b:512 * h + 128 * b + 128]).then_inc(S["tr%d" % s], 1)
+
+    def clamp(s):
+        V.wait_ge(S["xd%d" % s], 256)
+        for h in range(2):
+            V.tensor_scalar(T["p%d" % s][:, 512 * h:512 * h + 512], T["x%d" % s][:, h, :], T.ek[:, 0:1], None, O.max).then_inc(S["cl%d" % s], 1)
+        V.wait_ge(S["cl%d" % s], 2)
+        V.quantize_mx(T["pc%d" % s][:], T["ps%d" % s][:], T["p%d" % s][:]).then_inc(S["qz%d" % s], 1)
+
+    shift(0)
+    V.wait_ge(S.lv, 16)
+    V.quantize_mx(T.vc[:, 0:128], T.vs[:, 0:128], T.vt[:]).then_inc(S.vq, 1)
+    turn(0)
+    shift(1)
+    turn(1)
+    shift(2)
+    turn(2)
+    V.wait_ge(S.ek, 1)
+    clamp(1)
+    shift(3)
+    turn(3)
+    clamp(2)
+    clamp(0)
+    clamp(3)
+    for s in range(4):
+        for h in range(2):
+            V.wait_ge(S["nb%d%d" % (s, h)], 1)
+    V.wait_ge(S.mcw, 1)
+    V.tensor_scalar(T.cw[:, 0:8], T.nb[:], -1.0, None, O.mult).then_inc(S.cneg, 1)
+    V.tensor_copy(T.nbl[:, 8 * r:8 * r + 8], T.nb[:]).then_inc(S.cown, 1)
+    V.wait_ge(S.ca, sum(len(eng[i]) for i in others))
+    sh = lambda j: T.nbl[:, 8 * j + r:8 * j + 8:4]
+    V.tensor_tensor(T.mm[:, 0:2], T.nb[:, r:8:4], sh(mate), O.min).then_inc(S.mn0, 1)
+    V.tensor_tensor(T.mm[:, 8:10], sh(diag), sh(near), O.min).then_inc(S.mn1, 1)
+    V.wait_ge(S.mn0, 1)
+    V.wait_ge(S.mn1, 1)
+    V.tensor_tensor(T.mm[:, 16:18], T.mm[:, 0:2], T.mm[:, 8:10], O.min).then_inc(S.mn2, 1)
+    V.wait_ge(S.cneg, 1)
+    V.wait_ge(S.wx0, 1)
+    V.wait_ge(S.wx1, 1)
+    V.transpose(T.cwt[:], T.cw[:]).then_inc(S.cwt, 1)
+    V.wait_ge(S.ev0, 2)
+    for s in (1, 2):
+        V.wait_ge(S["tm%d" % s], 2)
+        V.tensor_tensor(T.acc[:], T.acc[:], T["tm%d" % s][:], O.add).then_inc(S["ad%d" % s], 1)
+        V.wait_ge(S["ad%d" % s], 1)
+    V.wait_ge(S["ra%d" % near], len(retm[near]))
+    V.tensor_scalar(T.tm3[:, RW:2 * RW], land(near, 1), wcol(near, 1), None, O.mult).then_inc(S.tm31, 1)
+    for h in range(2):
+        V.wait_ge(S["tm3%d" % h], 1)
+        a = T.acc[:, RW * h:RW * h + RW]
+        V.tensor_tensor(a, a, T.tm3[:, RW * h:RW * h + RW], O.add).then_inc(S["ad3%d" % h], 1)
+        V.wait_ge(S["ad3%d" % h], 1)
+        V.reciprocal(T.rd[:, 4 * h:4 * h + 1], T.acc[:, RW * h + 128:RW * h + 129]).then_inc(S["rc%d" % h], 1)
+        V.wait_ge(S["rc%d" % h], 1)
+        V.tensor_scalar(T.on[:, 128 * h:128 * h + 128], T.acc[:, RW * h:RW * h + 128], T.rd[:, 4 * h:4 * h + 1], None, O.mult).then_inc(S["nr%d" % h], 1)
+        V.wait_ge(S["nr%d" % h], 1)
+        V.transpose(T.ot[:, 128 * h:128 * h + 128], T.on[:, 128 * h:128 * h + 128]).then_inc(S["ott%d" % h], 1)
+
+    for s in range(3):
+        exchange(Y, s, blocks)
+    exchange(Y, 3, blocks[:8])
+    for s in (1, 2, 0, 3):
+        Y.wait_ge(S["cl%d" % s], 2)
+        Y.dma_start(T.p[rk[s]], T["p%d" % s][:]).then_inc(S.stp, 16)
+    Y.wait_ge(S.cwt, 1)
+    for h in range(2):
+        for a in range(4):
+            cs = slice(128 * h + 32 * a, 128 * h + 32 * a + 32)
+            Y.dma_start(T.c[:, cs], T.cwt[32 * a + 4 * h:32 * a + 4 * h + 4, :]).then_inc(S.stp, 16)
+            Y.dma_start(T.w[:, cs], T.cwt[32 * a + 8 + 4 * h:32 * a + 12 + 4 * h, :]).then_inc(S.stp, 16)
+    for q, h in ((Y, 0), (X, 1)):
+        q.wait_ge(S["ott%d" % h], 1)
+        for dq in range(4):
+            for tq in range(4):
+                q.dma_start(T.o[32 * dq:32 * dq + 32, 128 * h + 32 * tq:128 * h + 32 * tq + 32],
+                            T.ot[32 * tq:32 * tq + 32, 128 * h + 32 * dq:128 * h + 32 * dq + 32]).then_inc(S.sto if h else S.stp, 16)
+    Y.wait_ge(S.stp, 16 * (4 + 16 + 16))
+    X.wait_ge(S.sto, 16 * 16)

@@ -27,6 +27,7 @@ SCRATCH = {
     "cwt": ("sbuf", [128, 32], "float32"),
     "land": ("sbuf", [128, 4 * 2 * RW], "float32"),
     "acc": ("sbuf", [128, 2 * RW], "float32"),
+    "den": ("sbuf", [128, 8], "float32"),
     "rd": ("sbuf", [128, 8], "float32"),
     "on": ("sbuf", [128, 256], "float32"),
     "ot": ("sbuf", [128, 256], "float32"),
@@ -43,14 +44,15 @@ for _s in range(4):
 for _b in range(8):
     SCRATCH["bank%d" % _b] = ("psum", [128, 512], "float32")
 
-SEMAPHORES = ["lq", "lk0", "lk1", "lv", "m1", "mk", "mcw", "ek", "qq", "kq0", "kq1", "vq", "oq", "sent", "ca", "cneg", "cown",
-              "mn0", "mn1", "mn2", "wx0", "wx1", "cwt", "sto", "stp", "h1m"]
+SEMAPHORES = ["lq", "lv", "m1", "mk", "mcw", "ek", "qq", "vq", "oq", "sent", "ca", "cneg", "cown",
+              "mn0", "mn1", "mn2", "wx0", "wx1", "cwt", "sto", "stp"]
+SEMAPHORES += ["%s%d" % (a, b) for a in ("lk", "kq") for b in range(2)]
 for _s in range(4):
-    SEMAPHORES += ["qa%d" % _s, "ra%d" % _s, "tr%d" % _s, "xd%d" % _s, "cl%d" % _s, "qz%d" % _s, "ev%d" % _s, "tm%d" % _s, "ad%d" % _s]
+    SEMAPHORES += ["%s%d" % (a, _s) for a in ("qa", "ra")]
     for _h in range(2):
-        SEMAPHORES += ["st%d%d" % (_s, _h), "rm%d%d" % (_s, _h), "nb%d%d" % (_s, _h), "ex%d%d" % (_s, _h), "al%d%d" % (_s, _h)]
+        SEMAPHORES += ["%s%d%d" % (a, _s, _h) for a in ("st", "rm", "nb", "ex", "tr", "xd", "cl", "qz", "al", "ev", "tm", "ad")]
 for _h in range(2):
-    SEMAPHORES += ["ad3%d" % _h, "tm3%d" % _h, "rc%d" % _h, "nr%d" % _h, "ott%d" % _h]
+    SEMAPHORES += ["%s%d" % (a, _h) for a in ("rl", "dn", "rc", "nr", "ott")]
 
 
 def bits(mask):
@@ -69,164 +71,202 @@ def rank_program(g, core, T, topo):
     F = ActivationFunctionType
     O = AluOpType
     V, X, P, Y = g.vector, g.scalar, g.tensor, g.sync
+    HS = (0, 1)
     others = [i for i in range(N) if i != r]
     near = [i for i in others if topo.chip(T.cores[i]) == topo.chip(core)][0]
     far = [i for i in others if i != near]
     mate = [i for i in far if topo.die(T.cores[i]) == topo.die(core)][0]
     diag = [i for i in far if i != mate][0]
-    rk = [r, mate, diag, near]
+    rk = [r, near, mate, diag]
+    LAST = 3
     addr = {i: topo.addr(T.cores[i]) for i in others}
     off = bits(topo.mask(core, T.cores[mate]) & topo.mask(core, T.cores[diag]))
     on = bits(topo.mask(core, T.cores[near]))
     half = len(off) // 2
     eng = {mate: off[:half], diag: off[half:], near: [b for b in on if b not in off]}
-    retm = {mate: off, diag: off, near: on}
     sent = [0]
 
-    def tr(i, src, dst, sem):
-        sent[0] += len(eng[i])
-        return RemoteDMATransfer(dst_ids=[DstId(rid=addr[i][0], pnc=addr[i][1])], dma_engine_mask=to_mask(eng[i]), remote_sem=sem, src=src, dst=dst)
+    def sem(a, *k):
+        return S[a + "".join(str(x) for x in k)]
 
-    Y.dma_start(T.qt[:], T.q[:]).then_inc(S.lq, 16)
-    X.dma_start(T.kt[:, 0:1024], T.k[:, 0:1024]).then_inc(S.lk0, 16)
-    Y.dma_start(T.kt[:, 1024:2048], T.k[:, 1024:2048]).then_inc(S.lk1, 16)
-    X.dma_start(T.vt[:], T.v[:]).then_inc(S.lv, 16)
+    def tr(i, src, dst, rs):
+        sent[0] += len(eng[i])
+        return RemoteDMATransfer(dst_ids=[DstId(rid=addr[i][0], pnc=addr[i][1])], dma_engine_mask=to_mask(eng[i]), remote_sem=rs, src=src, dst=dst)
+
+    Y.dma_start(T.qt[:, 0:512], T.q[:, 0:512]).then_inc(S.lq, 16)
+    X.dma_start(T.qt[:, 512:1024], T.q[:, 512:1024]).then_inc(S.lq, 16)
+    Y.dma_start(T.kt[:, 0:1024], T.k[:, 0:1024]).then_inc(S.lk0, 16)
+    X.dma_start(T.kt[:, 1024:2048], T.k[:, 1024:2048]).then_inc(S.lk1, 16)
+    Y.dma_start(T.vt[:], T.v[:]).then_inc(S.lv, 16)
 
     sl = slice(NC * r, NC * r + NC)
     g.wait_ge(S.qq, 1)
-    g.remote_dma_fused([tr(i, T.qc[:, sl].bitcast(dt.uint8), T.qc[:, sl].bitcast(dt.uint8), S["qa%d" % r]) for i in (mate, diag, near)], local_sem=S.sent)
-    g.remote_dma_fused([tr(i, T.qs[:, sl], T.qs[:, sl], S["qa%d" % r]) for i in (mate, diag, near)], local_sem=S.sent)
+    g.remote_dma_fused([tr(i, T.qc[:, sl].bitcast(dt.uint8), T.qc[:, sl].bitcast(dt.uint8), sem("qa", r)) for i in (near, mate, diag)], local_sem=S.sent)
+    g.remote_dma_fused([tr(i, T.qs[:, sl], T.qs[:, sl], sem("qa", r)) for i in (near, mate, diag)], local_sem=S.sent)
     for s in range(4):
-        for h in range(2):
-            g.wait_ge(S["nb%d%d" % (s, h)], 1)
-    g.remote_dma_fused([tr(i, T.nb[:], T.nbl[:, 8 * r:8 * r + 8], S.ca) for i in (mate, diag, near)], local_sem=S.sent)
-    for s in (1, 2, 3):
+        for h in HS:
+            g.wait_ge(sem("nb", s, h), 1)
+    g.remote_dma_fused([tr(i, T.nb[:], T.nbl[:, 8 * r:8 * r + 8], S.ca) for i in (near, mate, diag)], local_sem=S.sent)
+
+    def home(s, c0, c1, rs):
         i = rk[s]
-        g.wait_ge(S["ev%d" % s], 2)
-        g.remote_dma(T["land"][:, 2 * RW * r:2 * RW * (r + 1)], T["r%d" % s][:], S["ra%d" % r], S.sent, addr[i][1], addr[i][0], to_mask(retm[i]))
-        sent[0] += len(retm[i])
+        m = bits(topo.mask(core, T.cores[i]))
+        g.remote_dma(T["land"][:, 2 * RW * r + c0:2 * RW * r + c1], T["r%d" % s][:, c0:c1], rs, S.sent, addr[i][1], addr[i][0], to_mask(m))
+        sent[0] += len(m)
+
+    for s in (1, 2):
+        for h in HS:
+            g.wait_ge(sem("ev", s, h), 1)
+        home(s, 0, 2 * RW, sem("ra", r))
+    for h in HS:
+        g.wait_ge(sem("ev", LAST, h), 1)
+        home(LAST, RW * h, RW * h + RW, sem("rl", h))
     g.wait_ge(S.sent, sent[0])
 
-    def scores(s):
+    for s in range(4):
         i = rk[s]
         if s == 0:
             P.wait_ge(S.qq, 1)
             P.wait_ge(S.kq0, 1)
             P.wait_ge(S.kq1, 1)
         else:
-            P.wait_ge(S["qa%d" % i], 2 * len(eng[i]))
-        for h in range(2):
+            P.wait_ge(sem("qa", i), 2 * len(eng[i]))
+        for h in HS:
             c0 = NC * i + 128 * h
-            P.matmul_mx(T["bank%d" % (2 * s + h)][:], T.qc[:, c0:c0 + 128], T.qs[:, c0:c0 + 128], T.kcd[:], T.ksc[:], True, True).then_inc(S["st%d%d" % (s, h)], 1)
-
-    albank = {1: 0, 2: 2, 0: 4, 3: 6}
-
-    def values(s):
-        b = albank[s]
-        P.wait_ge(S["qz%d" % s], 1)
-        for h in range(2):
-            P.wait_ge(S["ex%d%d" % (b // 2, h)], 1)
-            P.matmul_mx(T["bank%d" % (b + h)][:, 0:256], T["pc%d" % s][:, 128 * h:128 * h + 128], T["ps%d" % s][:, 128 * h:128 * h + 128],
-                        T.vc[:], T.vs[:], True, True).then_inc(S["al%d%d" % (s, h)], 1)
-
-    for s in range(4):
-        scores(s)
+            P.matmul_mx(T["bank%d" % (2 * s + h)][:], T.qc[:, c0:c0 + 128], T.qs[:, c0:c0 + 128], T.kcd[:], T.ksc[:], True, True).then_inc(sem("st", s, h), 1)
     P.wait_ge(S.vq, 1)
     P.wait_ge(S.oq, 1)
-    for s in (1, 2, 0, 3):
-        values(s)
+    albank = {1: 0, 0: 2, 2: 4, LAST: 6}
+    for s in (1, 0, 2, LAST):
+        for h in HS:
+            b = albank[s] + h
+            P.wait_ge(sem("qz", s, h if s == LAST else 0), 1)
+            P.wait_ge(sem("ex", b // 2, b % 2), 1)
+            P.matmul_mx(T["bank%d" % b][:, 0:256], T["pc%d" % s][:, 128 * h:128 * h + 128], T["ps%d" % s][:, 128 * h:128 * h + 128],
+                        T.vc[:], T.vs[:], True, True).then_inc(sem("al", s, h), 1)
 
     X.wait_ge(S.mk, 1)
     X.activation(T.ek[:, 0:1], T.kc[:, 0:1], F.Exp).then_inc(S.ek, 1)
     for s in range(4):
-        for h in range(2):
+        for h in HS:
             col = 4 * h + rk[s]
-            X.wait_ge(S["nb%d%d" % (s, h)], 1)
-            X.activation(T["e%d" % s][:, 512 * h:512 * h + 512], T["bank%d" % (2 * s + h)][:], F.Exp, bias=T.nb[:, col:col + 1], scale=A).then_inc(S["ex%d%d" % (s, h)], 1)
-
-    def exchange(q, s, pairs):
-        q.wait_ge(S["tr%d" % s], 8)
-        for kq, tq in pairs:
-            q.dma_start(T["x%d" % s][32 * kq:32 * kq + 32, :, 128 * tq:128 * tq + 128],
-                        T["i%d" % s][32 * tq:32 * tq + 32, :, 128 * kq:128 * kq + 128]).then_inc(S["xd%d" % s], 16)
-
+            X.wait_ge(sem("nb", s, h), 1)
+            X.activation(T["e%d" % s][:, 512 * h:512 * h + 512], T["bank%d" % (2 * s + h)][:], F.Exp, bias=T.nb[:, col:col + 1], scale=A).then_inc(sem("ex", s, h), 1)
     blocks = [(kq, tq) for kq in range(4) for tq in range(4)]
-    exchange(X, 3, blocks[8:])
-    for s in (1, 2, 3):
-        for h in range(2):
-            X.wait_ge(S["al%d%d" % (s, h)], 1)
-            X.activation(T["r%d" % s][:, RW * h:RW * h + RW], T["bank%d" % (albank[s] + h)][:, 0:RW], F.Copy).then_inc(S["ev%d" % s], 1)
+
+    def exchange(q, s, hs, pairs):
+        for h in hs:
+            q.wait_ge(sem("tr", s, h), 4)
+        h0, h1 = hs[0], hs[-1] + 1
+        for kq, tq in pairs:
+            q.dma_start(T["x%d" % s][32 * kq:32 * kq + 32, h0:h1, 128 * tq:128 * tq + 128],
+                        T["i%d" % s][32 * tq:32 * tq + 32, h0:h1, 128 * kq:128 * kq + 128]).then_inc(sem("xd", s, hs[-1]), 16)
+
+    CUT = 10
+    exchange(X, LAST, (1,), blocks[:CUT])
+
+    def evac(q, s, h, out, **k):
+        q.wait_ge(sem("al", s, h), 1)
+        src = T["bank%d" % (albank[s] + h)][:, 0:RW]
+        if q is V:
+            q.tensor_copy(out, src).then_inc(sem("ev", s, h), 1)
+        else:
+            q.activation(out, src, F.Copy, **k).then_inc(sem("ev", s, h), 1)
+
+    def part(b, h):
+        return b[:, RW * h:RW * h + RW]
+
+    for h in HS:
+        evac(X, 1, h, part(T.r1, h))
     wcol = lambda j, h: T.cw[:, 8 + 4 * h + j:9 + 4 * h + j]
     X.wait_ge(S.mn2, 1)
     X.wait_ge(S.cown, 1)
     X.wait_ge(S.mcw, 1)
-    for h in range(2):
-        X.activation(T.cw[:, 8 + 4 * h:12 + 4 * h], T.nbl[:, 4 * h + r:32:8], F.Exp, bias=T.mm[:, 16 + h:17 + h], scale=-1.0).then_inc(S["wx%d" % h], 1)
-    for h in range(2):
-        X.wait_ge(S["wx%d" % h], 1)
-        X.wait_ge(S["al0%d" % h], 1)
-        X.activation(T.acc[:, RW * h:RW * h + RW], T["bank%d" % (albank[0] + h)][:, 0:RW], F.Copy, scale=wcol(r, h)).then_inc(S.ev0, 1)
+    for h in HS:
+        X.activation(T.cw[:, 8 + 4 * h:12 + 4 * h], T.nbl[:, 4 * h + r:32:8], F.Exp, bias=T.mm[:, 16 + h:17 + h], scale=-1.0).then_inc(sem("wx", h), 1)
+    for h in HS:
+        X.wait_ge(sem("wx", h), 1)
+        evac(X, 0, h, part(T.acc, h), scale=wcol(r, h))
+    for h in HS:
+        evac(X, 2, h, part(T.r2, h))
+    evac(X, LAST, 0, part(T["r%d" % LAST], 0))
 
     def land(j, h):
         return T["land"][:, 2 * RW * j + RW * h:2 * RW * j + RW * h + RW]
 
+    def weigh(s, h):
+        X.activation(part(T["tm%d" % s], h), land(rk[s], h), F.Copy, scale=wcol(rk[s], h)).then_inc(sem("tm", s, h), 1)
+
+    arrived = lambda i: len(bits(topo.mask(core, T.cores[i])))
     for s in (1, 2):
-        X.wait_ge(S["ra%d" % rk[s]], len(retm[rk[s]]))
-        for h in range(2):
-            X.activation(T["tm%d" % s][:, RW * h:RW * h + RW], land(rk[s], h), F.Copy, scale=wcol(rk[s], h)).then_inc(S["tm%d" % s], 1)
-    X.wait_ge(S["ra%d" % near], len(retm[near]))
-    X.activation(T.tm3[:, 0:RW], land(near, 0), F.Copy, scale=wcol(near, 0)).then_inc(S.tm30, 1)
+        X.wait_ge(sem("ra", rk[s]), arrived(rk[s]))
+        for h in HS:
+            weigh(s, h)
+    for h in HS:
+        X.wait_ge(sem("rl", h), arrived(diag))
+        weigh(LAST, h)
 
     V.memset(T.one[:], 1.0).then_inc(S.m1, 1)
     V.memset(T.kc[:], -20.0).then_inc(S.mk, 1)
     V.memset(T.cw[:], 0.0).then_inc(S.mcw, 1)
     V.wait_ge(S.m1, 1)
     V.quantize_mx(T.vc[:, 128:256], T.vs[:, 128:256], T.one[:]).then_inc(S.oq, 1)
-    V.wait_ge(S.lq, 16)
+    V.wait_ge(S.lq, 32)
     V.quantize_mx(T.qc[:, sl], T.qs[:, sl], T.qt[:]).then_inc(S.qq, 1)
     for n in range(2):
-        V.wait_ge(S["lk%d" % n], 16)
-        V.quantize_mx(T.kcd[:, 256 * n:256 * n + 256], T.ksc[:, 256 * n:256 * n + 256], T.kt[:, 1024 * n:1024 * n + 1024]).then_inc(S["kq%d" % n], 1)
+        V.wait_ge(sem("lk", n), 16)
+        V.quantize_mx(T.kcd[:, 256 * n:256 * n + 256], T.ksc[:, 256 * n:256 * n + 256], T.kt[:, 1024 * n:1024 * n + 1024]).then_inc(sem("kq", n), 1)
 
-    def shift(s):
-        for h in range(2):
-            col = 4 * h + rk[s]
-            V.wait_ge(S["st%d%d" % (s, h)], 1)
-            V.tensor_reduce(T.nm[:, col:col + 1], T["bank%d" % (2 * s + h)][:], AxisListType.X, O.max, negate=True).then_inc(S["rm%d%d" % (s, h)], 1)
-            V.wait_ge(S["rm%d%d" % (s, h)], 1)
-            V.tensor_scalar(T.nb[:, col:col + 1], T.nm[:, col:col + 1], A, None, O.mult).then_inc(S["nb%d%d" % (s, h)], 1)
+    def shift(s, h):
+        col = 4 * h + rk[s]
+        V.wait_ge(sem("st", s, h), 1)
+        V.tensor_reduce(T.nm[:, col:col + 1], T["bank%d" % (2 * s + h)][:], AxisListType.X, O.max, negate=True).then_inc(sem("rm", s, h), 1)
+        V.wait_ge(sem("rm", s, h), 1)
+        V.tensor_scalar(T.nb[:, col:col + 1], T.nm[:, col:col + 1], A, None, O.mult).then_inc(sem("nb", s, h), 1)
 
-    def turn(s):
-        for h in range(2):
-            V.wait_ge(S["ex%d%d" % (s, h)], 1)
-            for b in range(4):
-                V.transpose(T["i%d" % s][:, h, b:512:4], T["e%d" % s][:, 512 * h + 128 * b:512 * h + 128 * b + 128]).then_inc(S["tr%d" % s], 1)
+    def turn(s, h):
+        V.wait_ge(sem("ex", s, h), 1)
+        for b in range(4):
+            V.transpose(T["i%d" % s][:, h, b:512:4], T["e%d" % s][:, 512 * h + 128 * b:512 * h + 128 * b + 128]).then_inc(sem("tr", s, h), 1)
 
-    def clamp(s):
-        V.wait_ge(S["xd%d" % s], 256)
-        for h in range(2):
-            V.tensor_scalar(T["p%d" % s][:, 512 * h:512 * h + 512], T["x%d" % s][:, h, :], T.ek[:, 0:1], None, O.max).then_inc(S["cl%d" % s], 1)
-        V.wait_ge(S["cl%d" % s], 2)
-        V.quantize_mx(T["pc%d" % s][:], T["ps%d" % s][:], T["p%d" % s][:]).then_inc(S["qz%d" % s], 1)
+    def clamp(s, h):
+        V.tensor_scalar(T["p%d" % s][:, 512 * h:512 * h + 512], T["x%d" % s][:, h, :], T.ek[:, 0:1], None, O.max).then_inc(sem("cl", s, h), 1)
 
-    shift(0)
+    def pack(s):
+        for h in HS:
+            V.wait_ge(sem("cl", s, h), 1)
+        V.quantize_mx(T["pc%d" % s][:], T["ps%d" % s][:], T["p%d" % s][:]).then_inc(sem("qz", s, 0), 1)
+
+    shift(0, 0)
+    shift(0, 1)
     V.wait_ge(S.lv, 16)
     V.quantize_mx(T.vc[:, 0:128], T.vs[:, 0:128], T.vt[:]).then_inc(S.vq, 1)
-    turn(0)
-    shift(1)
-    turn(1)
-    shift(2)
-    turn(2)
+    turn(0, 0)
+    turn(0, 1)
+    shift(1, 0)
+    shift(1, 1)
+    shift(2, 0)
+    turn(1, 0)
+    turn(1, 1)
+    shift(2, 1)
+    shift(3, 0)
+    turn(2, 0)
+    turn(2, 1)
+    shift(3, 1)
+    turn(3, 0)
     V.wait_ge(S.ek, 1)
-    clamp(1)
-    shift(3)
-    turn(3)
-    clamp(2)
-    clamp(0)
-    clamp(3)
+    V.wait_ge(sem("xd", 0, 1), 256)
+    clamp(0, 0)
+    turn(3, 1)
+    V.wait_ge(sem("xd", 1, 1), 256)
+    for h in HS:
+        clamp(1, h)
+    pack(1)
+    clamp(0, 1)
+    pack(0)
     for s in range(4):
-        for h in range(2):
-            V.wait_ge(S["nb%d%d" % (s, h)], 1)
+        for h in HS:
+            V.wait_ge(sem("nb", s, h), 1)
     V.wait_ge(S.mcw, 1)
     V.tensor_scalar(T.cw[:, 0:8], T.nb[:], -1.0, None, O.mult).then_inc(S.cneg, 1)
     V.tensor_copy(T.nbl[:, 8 * r:8 * r + 8], T.nb[:]).then_inc(S.cown, 1)
@@ -237,45 +277,72 @@ def rank_program(g, core, T, topo):
     V.wait_ge(S.mn0, 1)
     V.wait_ge(S.mn1, 1)
     V.tensor_tensor(T.mm[:, 16:18], T.mm[:, 0:2], T.mm[:, 8:10], O.min).then_inc(S.mn2, 1)
+    V.wait_ge(sem("xd", 2, 1), 256)
+    for h in HS:
+        clamp(2, h)
+    pack(2)
+    for h in HS:
+        V.wait_ge(sem("xd", LAST, h), 256)
+        clamp(LAST, h)
+        V.wait_ge(sem("cl", LAST, h), 1)
+        hs = slice(128 * h, 128 * h + 128)
+        V.quantize_mx(T["pc%d" % LAST][:, hs], T["ps%d" % LAST][:, hs], T["p%d" % LAST][:, 512 * h:512 * h + 512]).then_inc(sem("qz", LAST, h), 1)
     V.wait_ge(S.cneg, 1)
-    V.wait_ge(S.wx0, 1)
-    V.wait_ge(S.wx1, 1)
+    for h in HS:
+        V.wait_ge(sem("wx", h), 1)
     V.transpose(T.cwt[:], T.cw[:]).then_inc(S.cwt, 1)
-    V.wait_ge(S.ev0, 2)
-    for s in (1, 2):
-        V.wait_ge(S["tm%d" % s], 2)
-        V.tensor_tensor(T.acc[:], T.acc[:], T["tm%d" % s][:], O.add).then_inc(S["ad%d" % s], 1)
-        V.wait_ge(S["ad%d" % s], 1)
-    V.wait_ge(S["ra%d" % near], len(retm[near]))
-    V.tensor_scalar(T.tm3[:, RW:2 * RW], land(near, 1), wcol(near, 1), None, O.mult).then_inc(S.tm31, 1)
-    for h in range(2):
-        V.wait_ge(S["tm3%d" % h], 1)
-        a = T.acc[:, RW * h:RW * h + RW]
-        V.tensor_tensor(a, a, T.tm3[:, RW * h:RW * h + RW], O.add).then_inc(S["ad3%d" % h], 1)
-        V.wait_ge(S["ad3%d" % h], 1)
-        V.reciprocal(T.rd[:, 4 * h:4 * h + 1], T.acc[:, RW * h + 128:RW * h + 129]).then_inc(S["rc%d" % h], 1)
-        V.wait_ge(S["rc%d" % h], 1)
-        V.tensor_scalar(T.on[:, 128 * h:128 * h + 128], T.acc[:, RW * h:RW * h + 128], T.rd[:, 4 * h:4 * h + 1], None, O.mult).then_inc(S["nr%d" % h], 1)
-        V.wait_ge(S["nr%d" % h], 1)
-        V.transpose(T.ot[:, 128 * h:128 * h + 128], T.on[:, 128 * h:128 * h + 128]).then_inc(S["ott%d" % h], 1)
+    evac(V, LAST, 1, part(T["r%d" % LAST], 1))
+    for s in (1, 2, LAST):
+        for h in HS:
+            a = part(T.acc, h)
+            if s == LAST:
+                V.wait_ge(sem("rl", h), arrived(diag))
+                V.tensor_scalar(T.den[:, 4 * h:4 * h + 1], land(diag, h)[:, 128:129], wcol(diag, h), T.acc[:, RW * h + 128:RW * h + 129], O.mult, O.add).then_inc(sem("dn", h), 1)
+                V.wait_ge(sem("dn", h), 1)
+                V.reciprocal(T.rd[:, 4 * h:4 * h + 1], T.den[:, 4 * h:4 * h + 1]).then_inc(sem("rc", h), 1)
+                a = a[:, 0:128]
+            V.wait_ge(sem("tm", s, h), 1)
+            V.wait_ge(sem("ev", 0, h) if s == 1 else sem("ad", s - 1, h), 1)
+            V.tensor_tensor(a, a, part(T["tm%d" % s], h)[:, 0:128] if s == LAST else part(T["tm%d" % s], h), O.add).then_inc(sem("ad", s, h), 1)
+            if s == 2:
+                V.wait_ge(sem("ad", s, h), 1)
+    for h in HS:
+        oc = slice(128 * h, 128 * h + 128)
+        X.wait_ge(sem("ad", LAST, h), 1)
+        X.wait_ge(sem("rc", h), 1)
+        X.activation(T.on[:, oc], T.acc[:, RW * h:RW * h + 128], F.Copy, scale=T.rd[:, 4 * h:4 * h + 1]).then_inc(sem("nr", h), 1)
+        V.wait_ge(sem("nr", h), 1)
+        V.transpose(T.ot[:, oc], T.on[:, oc]).then_inc(sem("ott", h), 1)
 
     for s in range(3):
-        exchange(Y, s, blocks)
-    exchange(Y, 3, blocks[:8])
-    for s in (1, 2, 0, 3):
-        Y.wait_ge(S["cl%d" % s], 2)
+        exchange(Y, s, HS, blocks)
+    exchange(Y, LAST, (0,), blocks)
+    exchange(Y, LAST, (1,), blocks[CUT:])
+
+    def store_p(s):
+        for h in HS:
+            Y.wait_ge(sem("cl", s, h), 1)
         Y.dma_start(T.p[rk[s]], T["p%d" % s][:]).then_inc(S.stp, 16)
+
+    Y.wait_ge(sem("ev", LAST, 0), 1)
+    for s in (1, 0, 2, LAST):
+        store_p(s)
     Y.wait_ge(S.cwt, 1)
-    for h in range(2):
+    for h in HS:
         for a in range(4):
             cs = slice(128 * h + 32 * a, 128 * h + 32 * a + 32)
             Y.dma_start(T.c[:, cs], T.cwt[32 * a + 4 * h:32 * a + 4 * h + 4, :]).then_inc(S.stp, 16)
             Y.dma_start(T.w[:, cs], T.cwt[32 * a + 8 + 4 * h:32 * a + 12 + 4 * h, :]).then_inc(S.stp, 16)
-    for q, h in ((Y, 0), (X, 1)):
-        q.wait_ge(S["ott%d" % h], 1)
-        for dq in range(4):
-            for tq in range(4):
-                q.dma_start(T.o[32 * dq:32 * dq + 32, 128 * h + 32 * tq:128 * h + 32 * tq + 32],
-                            T.ot[32 * tq:32 * tq + 32, 128 * h + 32 * dq:128 * h + 32 * dq + 32]).then_inc(S.sto if h else S.stp, 16)
-    Y.wait_ge(S.stp, 16 * (4 + 16 + 16))
-    X.wait_ge(S.sto, 16 * 16)
+    oblocks = [(dq, tq) for dq in range(4) for tq in range(4)]
+
+    def store_o(q, h, bl, sm):
+        q.wait_ge(sem("ott", h), 1)
+        for dq, tq in bl:
+            q.dma_start(T.o[32 * dq:32 * dq + 32, 128 * h + 32 * tq:128 * h + 32 * tq + 32],
+                        T.ot[32 * tq:32 * tq + 32, 128 * h + 32 * dq:128 * h + 32 * dq + 32]).then_inc(sm, 16)
+
+    store_o(Y, 0, oblocks, S.stp)
+    store_o(X, 1, oblocks[:CUT], S.sto)
+    store_o(Y, 1, oblocks[CUT:], S.stp)
+    Y.wait_ge(S.stp, 16 * (4 + 16 + 32 - CUT))
+    X.wait_ge(S.sto, 16 * CUT)

@@ -23,29 +23,31 @@ SCRATCH = {
     "nb": ("sbuf", [128, 8], "float32"),
     "nbl": ("sbuf", [128, 32], "float32"),
     "mm": ("sbuf", [128, 24], "float32"),
+    "dd": ("sbuf", [128, 8], "float32"),
     "cw": ("sbuf", [128, 32], "float32"),
     "cwt": ("sbuf", [128, 32], "float32"),
+    "cwd": ("dram", [32, 4, 32], "float32"),
     "land": ("sbuf", [128, 4 * 2 * RW], "float32"),
     "acc": ("sbuf", [128, 2 * RW], "float32"),
-    "den": ("sbuf", [128, 8], "float32"),
-    "rd": ("sbuf", [128, 8], "float32"),
+    "rd": ("sbuf", [128, 16], "float32"),
     "on": ("sbuf", [128, 256], "float32"),
     "ot": ("sbuf", [128, 256], "float32"),
 }
 for _s in range(4):
     SCRATCH["e%d" % _s] = ("sbuf", [128, 1024], "bfloat16")
-    SCRATCH["i%d" % _s] = ("sbuf", [128, 2, 512], "bfloat16")
-    SCRATCH["x%d" % _s] = ("sbuf", [128, 2, 512], "bfloat16")
+    SCRATCH["i%d" % _s] = ("sbuf", [128, 1024], "bfloat16")
+    SCRATCH["x%d" % _s] = ("sbuf", [128, 8, 4, 32], "bfloat16")
     SCRATCH["p%d" % _s] = ("sbuf", [128, 1024], "bfloat16")
     SCRATCH["pc%d" % _s] = ("sbuf", [128, 256], "float8_e4m3fn_x4")
     SCRATCH["ps%d" % _s] = ("sbuf", [128, 256], "uint8")
-    SCRATCH["r%d" % _s] = ("sbuf", [128, 2 * RW], "float32")
-    SCRATCH["tm%d" % _s] = ("sbuf", [128, 2 * RW], "float32")
+    if _s:
+        SCRATCH["r%d" % _s] = ("sbuf", [128, 2 * RW], "float32")
+        SCRATCH["tm%d" % _s] = ("sbuf", [128, 2 * RW], "float32")
 for _b in range(8):
     SCRATCH["bank%d" % _b] = ("psum", [128, 512], "float32")
 
 SEMAPHORES = ["lq", "lv", "m1", "mk", "mcw", "ek", "qq", "vq", "oq", "sent", "ca", "cneg", "cown",
-              "mn0", "mn1", "mn2", "wx0", "wx1", "cwt", "sto", "stp"]
+              "mn0", "mn1", "mn2", "dd", "wx", "cwt", "cwd", "sto", "stp"]
 SEMAPHORES += ["%s%d" % (a, b) for a in ("lk", "kq") for b in range(2)]
 for _s in range(4):
     SEMAPHORES += ["%s%d" % (a, _s) for a in ("qa", "ra")]
@@ -93,11 +95,10 @@ def rank_program(g, core, T, topo):
         sent[0] += len(eng[i])
         return RemoteDMATransfer(dst_ids=[DstId(rid=addr[i][0], pnc=addr[i][1])], dma_engine_mask=to_mask(eng[i]), remote_sem=rs, src=src, dst=dst)
 
-    Y.dma_start(T.qt[:, 0:512], T.q[:, 0:512]).then_inc(S.lq, 16)
-    X.dma_start(T.qt[:, 512:1024], T.q[:, 512:1024]).then_inc(S.lq, 16)
-    Y.dma_start(T.kt[:, 0:1024], T.k[:, 0:1024]).then_inc(S.lk0, 16)
-    X.dma_start(T.kt[:, 1024:2048], T.k[:, 1024:2048]).then_inc(S.lk1, 16)
-    Y.dma_start(T.vt[:], T.v[:]).then_inc(S.lv, 16)
+    for buf, src, c0, w, s_ in ((T.qt, T.q, 0, 512, S.lq), (T.kt, T.k, 0, 512, S.lk0), (T.kt, T.k, 1024, 512, S.lk1), (T.vt, T.v, 0, 256, S.lv)):
+        for n, q in enumerate((Y, X)):
+            cs = slice(c0 + w * n, c0 + w * n + w)
+            q.dma_start(buf[:, cs], src[:, cs]).then_inc(s_, 16)
 
     sl = slice(NC * r, NC * r + NC)
     g.wait_ge(S.qq, 1)
@@ -136,8 +137,8 @@ def rank_program(g, core, T, topo):
             P.matmul_mx(T["bank%d" % (2 * s + h)][:], T.qc[:, c0:c0 + 128], T.qs[:, c0:c0 + 128], T.kcd[:], T.ksc[:], True, True).then_inc(sem("st", s, h), 1)
     P.wait_ge(S.vq, 1)
     P.wait_ge(S.oq, 1)
-    albank = {1: 0, 0: 2, 2: 4, LAST: 6}
-    for s in (1, 0, 2, LAST):
+    albank = {1: 0, 2: 2, LAST: 4, 0: 6}
+    for s in (1, 2, LAST, 0):
         for h in HS:
             b = albank[s] + h
             P.wait_ge(sem("qz", s, h if s == LAST else 0), 1)
@@ -149,62 +150,52 @@ def rank_program(g, core, T, topo):
     X.activation(T.ek[:, 0:1], T.kc[:, 0:1], F.Exp).then_inc(S.ek, 1)
     for s in range(4):
         for h in HS:
-            col = 4 * h + rk[s]
+            col = 2 * rk[s] + h
             X.wait_ge(sem("nb", s, h), 1)
             X.activation(T["e%d" % s][:, 512 * h:512 * h + 512], T["bank%d" % (2 * s + h)][:], F.Exp, bias=T.nb[:, col:col + 1], scale=A).then_inc(sem("ex", s, h), 1)
-    blocks = [(kq, tq) for kq in range(4) for tq in range(4)]
 
-    def exchange(q, s, hs, pairs):
-        for h in hs:
-            q.wait_ge(sem("tr", s, h), 4)
-        h0, h1 = hs[0], hs[-1] + 1
-        for kq, tq in pairs:
-            q.dma_start(T["x%d" % s][32 * kq:32 * kq + 32, h0:h1, 128 * tq:128 * tq + 128],
-                        T["i%d" % s][32 * tq:32 * tq + 32, h0:h1, 128 * kq:128 * kq + 128]).then_inc(sem("xd", s, hs[-1]), 16)
+    def exchange(q, s, h, quads=range(4)):
+        q.wait_ge(sem("tr", s, h), 4)
+        for tq in quads:
+            q.dma_start(T["x%d" % s][:, 4 * h + tq, :, :], T["i%d" % s][32 * tq:32 * tq + 32, 512 * h:512 * h + 512]).then_inc(sem("xd", s, h), 16)
 
-    CUT = 10
-    exchange(X, LAST, (1,), blocks[:CUT])
-
-    def evac(q, s, h, out, **k):
-        q.wait_ge(sem("al", s, h), 1)
-        src = T["bank%d" % (albank[s] + h)][:, 0:RW]
-        if q is V:
-            q.tensor_copy(out, src).then_inc(sem("ev", s, h), 1)
-        else:
-            q.activation(out, src, F.Copy, **k).then_inc(sem("ev", s, h), 1)
+    exchange(X, LAST, 1, (0, 1))
 
     def part(b, h):
         return b[:, RW * h:RW * h + RW]
 
-    for h in HS:
-        evac(X, 1, h, part(T.r1, h))
-    wcol = lambda j, h: T.cw[:, 8 + 4 * h + j:9 + 4 * h + j]
-    X.wait_ge(S.mn2, 1)
-    X.wait_ge(S.cown, 1)
-    X.wait_ge(S.mcw, 1)
-    for h in HS:
-        X.activation(T.cw[:, 8 + 4 * h:12 + 4 * h], T.nbl[:, 4 * h + r:32:8], F.Exp, bias=T.mm[:, 16 + h:17 + h], scale=-1.0).then_inc(sem("wx", h), 1)
-    for h in HS:
-        X.wait_ge(sem("wx", h), 1)
-        evac(X, 0, h, part(T.acc, h), scale=wcol(r, h))
-    for h in HS:
-        evac(X, 2, h, part(T.r2, h))
-    evac(X, LAST, 0, part(T["r%d" % LAST], 0))
+    def evac(q, s, h):
+        q.wait_ge(sem("al", s, h), 1)
+        src = T["bank%d" % (albank[s] + h)][:, 0:RW]
+        out = part(T["r%d" % s], h)
+        (q.tensor_copy(out, src) if q is V else q.activation(out, src, F.Copy)).then_inc(sem("ev", s, h), 1)
 
     def land(j, h):
         return T["land"][:, 2 * RW * j + RW * h:2 * RW * j + RW * h + RW]
 
-    def weigh(s, h):
-        X.activation(part(T["tm%d" % s], h), land(rk[s], h), F.Copy, scale=wcol(rk[s], h)).then_inc(sem("tm", s, h), 1)
+    def wcol(j, h):
+        return T.cw[:, 8 + 2 * j + h:9 + 2 * j + h]
 
     arrived = lambda i: len(bits(topo.mask(core, T.cores[i])))
-    for s in (1, 2):
-        X.wait_ge(sem("ra", rk[s]), arrived(rk[s]))
-        for h in HS:
-            weigh(s, h)
+
+    def weigh(q, s, h):
+        i = rk[s]
+        q.wait_ge(sem("rl", h) if s == LAST else sem("ra", i), arrived(i))
+        out = part(T["tm%d" % s], h)
+        (q.tensor_scalar(out, land(i, h), wcol(i, h), None, O.mult) if q is V else
+         q.activation(out, land(i, h), F.Copy, scale=wcol(i, h))).then_inc(sem("tm", s, h), 1)
+
     for h in HS:
-        X.wait_ge(sem("rl", h), arrived(diag))
-        weigh(LAST, h)
+        evac(X, 1, h)
+    for h in HS:
+        evac(X, 2, h)
+    X.wait_ge(S.dd, 2)
+    X.wait_ge(S.mcw, 1)
+    X.activation(T.cw[:, 8:16], T.dd[:], F.Exp, scale=-1.0).then_inc(S.wx, 1)
+    X.wait_ge(S.wx, 1)
+    for s in (1, LAST):
+        for h in HS:
+            weigh(X, s, h)
 
     V.memset(T.one[:], 1.0).then_inc(S.m1, 1)
     V.memset(T.kc[:], -20.0).then_inc(S.mk, 1)
@@ -214,11 +205,11 @@ def rank_program(g, core, T, topo):
     V.wait_ge(S.lq, 32)
     V.quantize_mx(T.qc[:, sl], T.qs[:, sl], T.qt[:]).then_inc(S.qq, 1)
     for n in range(2):
-        V.wait_ge(sem("lk", n), 16)
+        V.wait_ge(sem("lk", n), 32)
         V.quantize_mx(T.kcd[:, 256 * n:256 * n + 256], T.ksc[:, 256 * n:256 * n + 256], T.kt[:, 1024 * n:1024 * n + 1024]).then_inc(sem("kq", n), 1)
 
     def shift(s, h):
-        col = 4 * h + rk[s]
+        col = 2 * rk[s] + h
         V.wait_ge(sem("st", s, h), 1)
         V.tensor_reduce(T.nm[:, col:col + 1], T["bank%d" % (2 * s + h)][:], AxisListType.X, O.max, negate=True).then_inc(sem("rm", s, h), 1)
         V.wait_ge(sem("rm", s, h), 1)
@@ -226,123 +217,122 @@ def rank_program(g, core, T, topo):
 
     def turn(s, h):
         V.wait_ge(sem("ex", s, h), 1)
-        for b in range(4):
-            V.transpose(T["i%d" % s][:, h, b:512:4], T["e%d" % s][:, 512 * h + 128 * b:512 * h + 128 * b + 128]).then_inc(sem("tr", s, h), 1)
+        for B in range(4):
+            c0 = 512 * h + 128 * B
+            V.transpose(T["i%d" % s][:, c0:c0 + 128], T["e%d" % s][:, 512 * h + B:512 * h + 512:4]).then_inc(sem("tr", s, h), 1)
 
     def clamp(s, h):
-        V.tensor_scalar(T["p%d" % s][:, 512 * h:512 * h + 512], T["x%d" % s][:, h, :], T.ek[:, 0:1], None, O.max).then_inc(sem("cl", s, h), 1)
+        V.wait_ge(sem("xd", s, h), 64)
+        for b in range(4):
+            V.tensor_scalar(T["p%d" % s][:, 512 * h + b:512 * h + 512:4], T["x%d" % s][:, 4 * h:4 * h + 4, b, :], T.ek[:, 0:1], None, O.max).then_inc(sem("cl", s, h), 1)
 
-    def pack(s):
-        for h in HS:
-            V.wait_ge(sem("cl", s, h), 1)
-        V.quantize_mx(T["pc%d" % s][:], T["ps%d" % s][:], T["p%d" % s][:]).then_inc(sem("qz", s, 0), 1)
+    def pack(s, hs=HS):
+        for h in hs:
+            V.wait_ge(sem("cl", s, h), 4)
+        a, b = 128 * hs[0], 128 * hs[-1] + 128
+        V.quantize_mx(T["pc%d" % s][:, a:b], T["ps%d" % s][:, a:b], T["p%d" % s][:, 4 * a:4 * b]).then_inc(sem("qz", s, hs[0]), 1)
 
-    shift(0, 0)
-    shift(0, 1)
-    V.wait_ge(S.lv, 16)
+    pieces = [(s, h) for s in range(4) for h in HS]
+    shift(*pieces[0])
+    shift(*pieces[1])
+    V.wait_ge(S.lv, 32)
     V.quantize_mx(T.vc[:, 0:128], T.vs[:, 0:128], T.vt[:]).then_inc(S.vq, 1)
-    turn(0, 0)
-    turn(0, 1)
-    shift(1, 0)
-    shift(1, 1)
-    shift(2, 0)
-    turn(1, 0)
-    turn(1, 1)
-    shift(2, 1)
-    shift(3, 0)
-    turn(2, 0)
-    turn(2, 1)
-    shift(3, 1)
-    turn(3, 0)
+    for n in range(6):
+        turn(*pieces[n])
+        shift(*pieces[n + 2])
+    turn(LAST, 0)
     V.wait_ge(S.ek, 1)
-    V.wait_ge(sem("xd", 0, 1), 256)
     clamp(0, 0)
-    turn(3, 1)
-    V.wait_ge(sem("xd", 1, 1), 256)
-    for h in HS:
-        clamp(1, h)
-    pack(1)
-    clamp(0, 1)
-    pack(0)
+    turn(LAST, 1)
+    for s in (1, 2):
+        for h in HS:
+            clamp(s, h)
+        pack(s)
+    clamp(LAST, 0)
+    pack(LAST, (0,))
     for s in range(4):
         for h in HS:
             V.wait_ge(sem("nb", s, h), 1)
-    V.wait_ge(S.mcw, 1)
-    V.tensor_scalar(T.cw[:, 0:8], T.nb[:], -1.0, None, O.mult).then_inc(S.cneg, 1)
     V.tensor_copy(T.nbl[:, 8 * r:8 * r + 8], T.nb[:]).then_inc(S.cown, 1)
     V.wait_ge(S.ca, sum(len(eng[i]) for i in others))
-    sh = lambda j: T.nbl[:, 8 * j + r:8 * j + 8:4]
-    V.tensor_tensor(T.mm[:, 0:2], T.nb[:, r:8:4], sh(mate), O.min).then_inc(S.mn0, 1)
+    sh = lambda j: T.nbl[:, 8 * j + 2 * r:8 * j + 2 * r + 2]
+    V.tensor_tensor(T.mm[:, 0:2], T.nb[:, 2 * r:2 * r + 2], sh(mate), O.min).then_inc(S.mn0, 1)
     V.tensor_tensor(T.mm[:, 8:10], sh(diag), sh(near), O.min).then_inc(S.mn1, 1)
     V.wait_ge(S.mn0, 1)
     V.wait_ge(S.mn1, 1)
     V.tensor_tensor(T.mm[:, 16:18], T.mm[:, 0:2], T.mm[:, 8:10], O.min).then_inc(S.mn2, 1)
-    V.wait_ge(sem("xd", 2, 1), 256)
+    V.wait_ge(S.mn2, 1)
+    V.wait_ge(S.cown, 1)
     for h in HS:
-        clamp(2, h)
-    pack(2)
-    for h in HS:
-        V.wait_ge(sem("xd", LAST, h), 256)
-        clamp(LAST, h)
-        V.wait_ge(sem("cl", LAST, h), 1)
-        hs = slice(128 * h, 128 * h + 128)
-        V.quantize_mx(T["pc%d" % LAST][:, hs], T["ps%d" % LAST][:, hs], T["p%d" % LAST][:, 512 * h:512 * h + 512]).then_inc(sem("qz", LAST, h), 1)
+        V.tensor_scalar(T.dd[:, h:8:2], T.nbl[:, 2 * r + h:32:8], T.mm[:, 16 + h:17 + h], None, O.subtract).then_inc(S.dd, 1)
+    evac(V, LAST, 0)
+    clamp(LAST, 1)
+    pack(LAST, (1,))
+    clamp(0, 1)
+    evac(V, LAST, 1)
+    pack(0)
+    V.wait_ge(S.mcw, 1)
+    V.tensor_scalar(T.cw[:, 0:8], T.nb[:], -1.0, None, O.mult).then_inc(S.cneg, 1)
     V.wait_ge(S.cneg, 1)
-    for h in HS:
-        V.wait_ge(sem("wx", h), 1)
+    V.wait_ge(S.wx, 1)
     V.transpose(T.cwt[:], T.cw[:]).then_inc(S.cwt, 1)
-    evac(V, LAST, 1, part(T["r%d" % LAST], 1))
+    for h in HS:
+        V.wait_ge(sem("al", 0, h), 1)
+        V.tensor_scalar(part(T.acc, h), T["bank%d" % (albank[0] + h)][:, 0:RW], wcol(r, h), None, O.mult).then_inc(sem("ev", 0, h), 1)
     for s in (1, 2, LAST):
+        if s == 2:
+            for h in HS:
+                weigh(V, 2, h)
         for h in HS:
             a = part(T.acc, h)
             if s == LAST:
+                V.wait_ge(sem("ad", 2, h), 1)
                 V.wait_ge(sem("rl", h), arrived(diag))
-                V.tensor_scalar(T.den[:, 4 * h:4 * h + 1], land(diag, h)[:, 128:129], wcol(diag, h), T.acc[:, RW * h + 128:RW * h + 129], O.mult, O.add).then_inc(sem("dn", h), 1)
+                V.tensor_scalar(T.rd[:, 4 * h:4 * h + 1], land(diag, h)[:, 128:129], wcol(diag, h), T.acc[:, RW * h + 128:RW * h + 129], O.mult, O.add).then_inc(sem("dn", h), 1)
                 V.wait_ge(sem("dn", h), 1)
-                V.reciprocal(T.rd[:, 4 * h:4 * h + 1], T.den[:, 4 * h:4 * h + 1]).then_inc(sem("rc", h), 1)
+                V.reciprocal(T.rd[:, 8 + 4 * h:9 + 4 * h], T.rd[:, 4 * h:4 * h + 1]).then_inc(sem("rc", h), 1)
                 a = a[:, 0:128]
             V.wait_ge(sem("tm", s, h), 1)
             V.wait_ge(sem("ev", 0, h) if s == 1 else sem("ad", s - 1, h), 1)
             V.tensor_tensor(a, a, part(T["tm%d" % s], h)[:, 0:128] if s == LAST else part(T["tm%d" % s], h), O.add).then_inc(sem("ad", s, h), 1)
-            if s == 2:
-                V.wait_ge(sem("ad", s, h), 1)
+
+    def scaled(q, h):
+        q.wait_ge(sem("ad", LAST, h), 1)
+        q.wait_ge(sem("rc", h), 1)
+        out, a, f = T.on[:, 128 * h:128 * h + 128], T.acc[:, RW * h:RW * h + 128], T.rd[:, 8 + 4 * h:9 + 4 * h]
+        (q.tensor_scalar(out, a, f, None, O.mult) if q is V else q.activation(out, a, F.Copy, scale=f)).then_inc(sem("nr", h), 1)
+
+    scaled(X, 0)
+    scaled(V, 1)
     for h in HS:
-        oc = slice(128 * h, 128 * h + 128)
-        X.wait_ge(sem("ad", LAST, h), 1)
-        X.wait_ge(sem("rc", h), 1)
-        X.activation(T.on[:, oc], T.acc[:, RW * h:RW * h + 128], F.Copy, scale=T.rd[:, 4 * h:4 * h + 1]).then_inc(sem("nr", h), 1)
         V.wait_ge(sem("nr", h), 1)
-        V.transpose(T.ot[:, oc], T.on[:, oc]).then_inc(sem("ott", h), 1)
+        for B in range(4):
+            c0 = 128 * h + 32 * B
+            V.transpose(T.ot[:, c0:c0 + 32], T.on[:, 128 * h + B:128 * h + 128:4]).then_inc(sem("ott", h), 1)
 
-    for s in range(3):
-        exchange(Y, s, HS, blocks)
-    exchange(Y, LAST, (0,), blocks)
-    exchange(Y, LAST, (1,), blocks[CUT:])
-
-    def store_p(s):
-        for h in HS:
-            Y.wait_ge(sem("cl", s, h), 1)
-        Y.dma_start(T.p[rk[s]], T["p%d" % s][:]).then_inc(S.stp, 16)
-
+    for s, h in pieces[:-1]:
+        exchange(Y, s, h)
+    exchange(Y, LAST, 1, (2, 3))
     Y.wait_ge(sem("ev", LAST, 0), 1)
-    for s in (1, 0, 2, LAST):
-        store_p(s)
+    for s in (1, 2, LAST, 0):
+        for h in HS:
+            Y.wait_ge(sem("cl", s, h), 4)
+        Y.dma_start(T.p[rk[s]], T["p%d" % s][:]).then_inc(S.stp, 16)
     Y.wait_ge(S.cwt, 1)
-    for h in HS:
-        for a in range(4):
-            cs = slice(128 * h + 32 * a, 128 * h + 32 * a + 32)
-            Y.dma_start(T.c[:, cs], T.cwt[32 * a + 4 * h:32 * a + 4 * h + 4, :]).then_inc(S.stp, 16)
-            Y.dma_start(T.w[:, cs], T.cwt[32 * a + 8 + 4 * h:32 * a + 12 + 4 * h, :]).then_inc(S.stp, 16)
-    oblocks = [(dq, tq) for dq in range(4) for tq in range(4)]
+    for a in range(4):
+        Y.dma_start(T.cwd[:, a, :], T.cwt[32 * a:32 * a + 32, :]).then_inc(S.cwd, 16)
+    Y.wait_ge(S.cwd, 64)
+    Y.dma_start(T.c[:, :], T.cwd[0:8, :, :]).then_inc(S.stp, 16)
+    Y.dma_start(T.w[:, :], T.cwd[8:16, :, :]).then_inc(S.stp, 16)
 
-    def store_o(q, h, bl, sm):
-        q.wait_ge(sem("ott", h), 1)
-        for dq, tq in bl:
-            q.dma_start(T.o[32 * dq:32 * dq + 32, 128 * h + 32 * tq:128 * h + 32 * tq + 32],
-                        T.ot[32 * tq:32 * tq + 32, 128 * h + 32 * dq:128 * h + 32 * dq + 32]).then_inc(sm, 16)
+    def store_o(q, h, quads, sm):
+        q.wait_ge(sem("ott", h), 4)
+        for tq in quads:
+            q.dma_start(T.o[:, 128 * h + 32 * tq:128 * h + 32 * tq + 32], T.ot[32 * tq:32 * tq + 32, 128 * h:128 * h + 128]).then_inc(sm, 16)
 
-    store_o(Y, 0, oblocks, S.stp)
-    store_o(X, 1, oblocks[:CUT], S.sto)
-    store_o(Y, 1, oblocks[CUT:], S.stp)
-    Y.wait_ge(S.stp, 16 * (4 + 16 + 32 - CUT))
-    X.wait_ge(S.sto, 16 * CUT)
+    store_o(Y, 0, (0, 1), S.stp)
+    store_o(X, 0, (2, 3), S.sto)
+    store_o(Y, 1, (0, 1), S.stp)
+    store_o(X, 1, (2, 3), S.sto)
+    Y.wait_ge(S.stp, 16 * 10)
+    X.wait_ge(S.sto, 16 * 4)

@@ -22,8 +22,7 @@ SCRATCH = {
     "nm": ("sbuf", [128, 8], "float32"),
     "nb": ("sbuf", [128, 8], "float32"),
     "nbl": ("sbuf", [128, 32], "float32"),
-    "mm": ("sbuf", [128, 24], "float32"),
-    "dd": ("sbuf", [128, 8], "float32"),
+    "mm": ("sbuf", [128, 8], "float32"),
     "cw": ("sbuf", [128, 32], "float32"),
     "cwt": ("sbuf", [128, 32], "float32"),
     "cwd": ("dram", [32, 4, 32], "float32"),
@@ -36,7 +35,7 @@ SCRATCH = {
 for _s in range(4):
     SCRATCH["e%d" % _s] = ("sbuf", [128, 1024], "bfloat16")
     SCRATCH["i%d" % _s] = ("sbuf", [128, 1024], "bfloat16")
-    SCRATCH["x%d" % _s] = ("sbuf", [128, 8, 4, 32], "bfloat16")
+    SCRATCH["x%d" % _s] = ("sbuf", [128, 4, 8, 32], "bfloat16")
     SCRATCH["p%d" % _s] = ("sbuf", [128, 1024], "bfloat16")
     SCRATCH["pc%d" % _s] = ("sbuf", [128, 256], "float8_e4m3fn_x4")
     SCRATCH["ps%d" % _s] = ("sbuf", [128, 256], "uint8")
@@ -47,14 +46,14 @@ for _b in range(8):
     SCRATCH["bank%d" % _b] = ("psum", [128, 512], "float32")
 
 SEMAPHORES = ["lq", "lv", "m1", "mk", "mcw", "ek", "qq", "vq", "oq", "sent", "ca", "cneg", "cown",
-              "mn0", "mn1", "mn2", "dd", "wx", "cwt", "cwd", "sto", "stp"]
+              "mm", "wx", "cwt", "cwd", "sto", "stp", "dn", "rc"]
 SEMAPHORES += ["%s%d" % (a, b) for a in ("lk", "kq") for b in range(2)]
 for _s in range(4):
     SEMAPHORES += ["%s%d" % (a, _s) for a in ("qa", "ra")]
     for _h in range(2):
         SEMAPHORES += ["%s%d%d" % (a, _s, _h) for a in ("st", "rm", "nb", "ex", "tr", "xd", "cl", "qz", "al", "ev", "tm", "ad")]
 for _h in range(2):
-    SEMAPHORES += ["%s%d" % (a, _h) for a in ("rl", "dn", "rc", "nr", "ott")]
+    SEMAPHORES += ["%s%d" % (a, _h) for a in ("rl", "nr", "ott")]
 
 
 def bits(mask):
@@ -85,15 +84,20 @@ def rank_program(g, core, T, topo):
     off = bits(topo.mask(core, T.cores[mate]) & topo.mask(core, T.cores[diag]))
     on = bits(topo.mask(core, T.cores[near]))
     half = len(off) // 2
-    eng = {mate: off[:half], diag: off[half:], near: [b for b in on if b not in off]}
+    inner = [b for b in on if b not in off]
+    qeng = {near: inner, mate: off, diag: off}
+    eng = {near: inner, mate: off[:half], diag: off[half:]}
     sent = [0]
 
     def sem(a, *k):
         return S[a + "".join(str(x) for x in k)]
 
-    def tr(i, src, dst, rs):
-        sent[0] += len(eng[i])
-        return RemoteDMATransfer(dst_ids=[DstId(rid=addr[i][0], pnc=addr[i][1])], dma_engine_mask=to_mask(eng[i]), remote_sem=rs, src=src, dst=dst)
+    def shifted(s, h):
+        return sem("nb", s, 0 if s in (1, 2) else h)
+
+    def tr(i, src, dst, rs, es):
+        sent[0] += len(es[i])
+        return RemoteDMATransfer(dst_ids=[DstId(rid=addr[i][0], pnc=addr[i][1])], dma_engine_mask=to_mask(es[i]), remote_sem=rs, src=src, dst=dst)
 
     for buf, src, c0, w, s_ in ((T.qt, T.q, 0, 512, S.lq), (T.kt, T.k, 0, 512, S.lk0), (T.kt, T.k, 1024, 512, S.lk1), (T.vt, T.v, 0, 256, S.lv)):
         for n, q in enumerate((Y, X)):
@@ -102,12 +106,13 @@ def rank_program(g, core, T, topo):
 
     sl = slice(NC * r, NC * r + NC)
     g.wait_ge(S.qq, 1)
-    g.remote_dma_fused([tr(i, T.qc[:, sl].bitcast(dt.uint8), T.qc[:, sl].bitcast(dt.uint8), sem("qa", r)) for i in (near, mate, diag)], local_sem=S.sent)
-    g.remote_dma_fused([tr(i, T.qs[:, sl], T.qs[:, sl], sem("qa", r)) for i in (near, mate, diag)], local_sem=S.sent)
+    for to in ((near, mate), (diag,)):
+        g.remote_dma_fused([tr(i, T.qc[:, sl].bitcast(dt.uint8), T.qc[:, sl].bitcast(dt.uint8), sem("qa", r), qeng) for i in to], local_sem=S.sent)
+        g.remote_dma_fused([tr(i, T.qs[:, sl], T.qs[:, sl], sem("qa", r), qeng) for i in to], local_sem=S.sent)
     for s in range(4):
         for h in HS:
-            g.wait_ge(sem("nb", s, h), 1)
-    g.remote_dma_fused([tr(i, T.nb[:], T.nbl[:, 8 * r:8 * r + 8], S.ca) for i in (near, mate, diag)], local_sem=S.sent)
+            g.wait_ge(shifted(s, h), 1)
+    g.remote_dma_fused([tr(i, T.nb[:], T.nbl[:, 8 * r:8 * r + 8], S.ca, eng) for i in (near, mate, diag)], local_sem=S.sent)
 
     def home(s, c0, c1, rs):
         i = rk[s]
@@ -131,7 +136,7 @@ def rank_program(g, core, T, topo):
             P.wait_ge(S.kq0, 1)
             P.wait_ge(S.kq1, 1)
         else:
-            P.wait_ge(sem("qa", i), 2 * len(eng[i]))
+            P.wait_ge(sem("qa", i), 2 * len(qeng[i]))
         for h in HS:
             c0 = NC * i + 128 * h
             P.matmul_mx(T["bank%d" % (2 * s + h)][:], T.qc[:, c0:c0 + 128], T.qs[:, c0:c0 + 128], T.kcd[:], T.ksc[:], True, True).then_inc(sem("st", s, h), 1)
@@ -151,15 +156,21 @@ def rank_program(g, core, T, topo):
     for s in range(4):
         for h in HS:
             col = 2 * rk[s] + h
-            X.wait_ge(sem("nb", s, h), 1)
+            X.wait_ge(shifted(s, h), 1)
             X.activation(T["e%d" % s][:, 512 * h:512 * h + 512], T["bank%d" % (2 * s + h)][:], F.Exp, bias=T.nb[:, col:col + 1], scale=A).then_inc(sem("ex", s, h), 1)
 
-    def exchange(q, s, h, quads=range(4)):
-        q.wait_ge(sem("tr", s, h), 4)
+    def exchange(q, s, h=0, quads=range(4)):
+        q.wait_ge(sem("tr", s, h), 4 if s else 8)
         for tq in quads:
-            q.dma_start(T["x%d" % s][:, 4 * h + tq, :, :], T["i%d" % s][32 * tq:32 * tq + 32, 512 * h:512 * h + 512]).then_inc(sem("xd", s, h), 16)
+            rows = slice(32 * tq, 32 * tq + 32)
+            if s == LAST:
+                q.dma_start(T["x%d" % s][:, tq, 4 * h:4 * h + 4, :], T["i%d" % s][rows, 512 * h:512 * h + 512]).then_inc(sem("xd", s, h), 16)
+            else:
+                q.dma_start(T["x%d" % s][:, tq, :, :], T["i%d" % s][rows, :]).then_inc(sem("xd", s, 0), 16)
 
     exchange(X, LAST, 1, (0, 1))
+    X.wait_ge(S.mcw, 1)
+    X.activation(T.cw[:, 0:8], T.nb[:], F.Copy, scale=-1.0).then_inc(S.cneg, 1)
 
     def part(b, h):
         return b[:, RW * h:RW * h + RW]
@@ -185,17 +196,17 @@ def rank_program(g, core, T, topo):
         (q.tensor_scalar(out, land(i, h), wcol(i, h), None, O.mult) if q is V else
          q.activation(out, land(i, h), F.Copy, scale=wcol(i, h))).then_inc(sem("tm", s, h), 1)
 
-    for h in HS:
-        evac(X, 1, h)
-    for h in HS:
-        evac(X, 2, h)
-    X.wait_ge(S.dd, 2)
-    X.wait_ge(S.mcw, 1)
-    X.activation(T.cw[:, 8:16], T.dd[:], F.Exp, scale=-1.0).then_inc(S.wx, 1)
-    X.wait_ge(S.wx, 1)
-    for s in (1, LAST):
+    for s in (1, 2):
         for h in HS:
-            weigh(X, s, h)
+            evac(X, s, h)
+    X.wait_ge(S.mm, 2)
+    for h in HS:
+        X.activation(T.cw[:, 8 + h:16:2], T.nbl[:, 2 * r + h:32:8], F.Exp, bias=T.mm[:, h:h + 1], scale=-1.0).then_inc(S.wx, 1)
+    X.wait_ge(S.wx, 2)
+    for s in (1, 2, LAST):
+        for h in HS:
+            if (s, h) != (2, 1):
+                weigh(X, s, h)
 
     V.memset(T.one[:], 1.0).then_inc(S.m1, 1)
     V.memset(T.kc[:], -20.0).then_inc(S.mk, 1)
@@ -208,23 +219,32 @@ def rank_program(g, core, T, topo):
         V.wait_ge(sem("lk", n), 32)
         V.quantize_mx(T.kcd[:, 256 * n:256 * n + 256], T.ksc[:, 256 * n:256 * n + 256], T.kt[:, 1024 * n:1024 * n + 1024]).then_inc(sem("kq", n), 1)
 
-    def shift(s, h):
-        col = 2 * rk[s] + h
-        V.wait_ge(sem("st", s, h), 1)
-        V.tensor_reduce(T.nm[:, col:col + 1], T["bank%d" % (2 * s + h)][:], AxisListType.X, O.max, negate=True).then_inc(sem("rm", s, h), 1)
-        V.wait_ge(sem("rm", s, h), 1)
-        V.tensor_scalar(T.nb[:, col:col + 1], T.nm[:, col:col + 1], A, None, O.mult).then_inc(sem("nb", s, h), 1)
+    def shift(s, *hs):
+        col = 2 * rk[s] + hs[0]
+        for n, h in enumerate(hs):
+            V.wait_ge(sem("st", s, h), 1)
+            V.tensor_reduce(T.nm[:, col + n:col + n + 1], T["bank%d" % (2 * s + h)][:], AxisListType.X, O.max, negate=True).then_inc(sem("rm", s, h), 1)
+        for h in hs:
+            V.wait_ge(sem("rm", s, h), 1)
+        V.tensor_scalar(T.nb[:, col:col + len(hs)], T.nm[:, col:col + len(hs)], A, None, O.mult).then_inc(shifted(s, hs[0]), 1)
 
-    def turn(s, h):
-        V.wait_ge(sem("ex", s, h), 1)
+    def turn(s, hs=HS):
+        for h in hs:
+            V.wait_ge(sem("ex", s, h), 1)
+        w = 128 * len(hs)
         for B in range(4):
-            c0 = 512 * h + 128 * B
-            V.transpose(T["i%d" % s][:, c0:c0 + 128], T["e%d" % s][:, 512 * h + B:512 * h + 512:4]).then_inc(sem("tr", s, h), 1)
+            c0 = 512 * hs[0]
+            V.transpose(T["i%d" % s][:, c0 + w * B:c0 + w * B + w], T["e%d" % s][:, c0 + B:c0 + 4 * w:4]).then_inc(sem("tr", s, hs[0]), 1)
+
+    def turn_own(h):
+        V.wait_ge(sem("ex", 0, h), 1)
+        for B in range(4):
+            V.transpose(T.i0[:, 256 * B + 128 * h:256 * B + 128 * h + 128], T.e0[:, 512 * h + B:512 * h + 512:4]).then_inc(sem("tr", 0, 0), 1)
 
     def clamp(s, h):
-        V.wait_ge(sem("xd", s, h), 64)
+        V.wait_ge(sem("xd", s, h if s == LAST else 0), 64)
         for b in range(4):
-            V.tensor_scalar(T["p%d" % s][:, 512 * h + b:512 * h + 512:4], T["x%d" % s][:, 4 * h:4 * h + 4, b, :], T.ek[:, 0:1], None, O.max).then_inc(sem("cl", s, h), 1)
+            V.tensor_scalar(T["p%d" % s][:, 512 * h + b:512 * h + 512:4], T["x%d" % s][:, :, 4 * h + b, :], T.ek[:, 0:1], None, O.max).then_inc(sem("cl", s, h), 1)
 
     def pack(s, hs=HS):
         for h in hs:
@@ -232,74 +252,76 @@ def rank_program(g, core, T, topo):
         a, b = 128 * hs[0], 128 * hs[-1] + 128
         V.quantize_mx(T["pc%d" % s][:, a:b], T["ps%d" % s][:, a:b], T["p%d" % s][:, 4 * a:4 * b]).then_inc(sem("qz", s, hs[0]), 1)
 
-    pieces = [(s, h) for s in range(4) for h in HS]
-    shift(*pieces[0])
-    shift(*pieces[1])
+    shift(0, 0)
+    shift(0, 1)
     V.wait_ge(S.lv, 32)
     V.quantize_mx(T.vc[:, 0:128], T.vs[:, 0:128], T.vt[:]).then_inc(S.vq, 1)
-    for n in range(6):
-        turn(*pieces[n])
-        shift(*pieces[n + 2])
-    turn(LAST, 0)
+    turn_own(0)
+    shift(1, 0, 1)
+    turn_own(1)
+    shift(2, 0, 1)
+    turn(1)
+    shift(LAST, 0)
+    turn(2)
+    shift(LAST, 1)
+    turn(LAST, (0,))
     V.wait_ge(S.ek, 1)
     clamp(0, 0)
-    turn(LAST, 1)
-    for s in (1, 2):
-        for h in HS:
-            clamp(s, h)
-        pack(s)
+    turn(LAST, (1,))
+    for h in HS:
+        clamp(1, h)
+    pack(1)
+    clamp(0, 1)
+    for h in HS:
+        clamp(2, h)
+    pack(2)
     clamp(LAST, 0)
     pack(LAST, (0,))
     for s in range(4):
         for h in HS:
-            V.wait_ge(sem("nb", s, h), 1)
+            V.wait_ge(shifted(s, h), 1)
     V.tensor_copy(T.nbl[:, 8 * r:8 * r + 8], T.nb[:]).then_inc(S.cown, 1)
     V.wait_ge(S.ca, sum(len(eng[i]) for i in others))
-    sh = lambda j: T.nbl[:, 8 * j + 2 * r:8 * j + 2 * r + 2]
-    V.tensor_tensor(T.mm[:, 0:2], T.nb[:, 2 * r:2 * r + 2], sh(mate), O.min).then_inc(S.mn0, 1)
-    V.tensor_tensor(T.mm[:, 8:10], sh(diag), sh(near), O.min).then_inc(S.mn1, 1)
-    V.wait_ge(S.mn0, 1)
-    V.wait_ge(S.mn1, 1)
-    V.tensor_tensor(T.mm[:, 16:18], T.mm[:, 0:2], T.mm[:, 8:10], O.min).then_inc(S.mn2, 1)
-    V.wait_ge(S.mn2, 1)
     V.wait_ge(S.cown, 1)
     for h in HS:
-        V.tensor_scalar(T.dd[:, h:8:2], T.nbl[:, 2 * r + h:32:8], T.mm[:, 16 + h:17 + h], None, O.subtract).then_inc(S.dd, 1)
-    evac(V, LAST, 0)
+        V.tensor_reduce(T.mm[:, h:h + 1], T.nbl[:, 2 * r + h:32:8], AxisListType.X, O.min).then_inc(S.mm, 1)
     clamp(LAST, 1)
     pack(LAST, (1,))
-    clamp(0, 1)
-    evac(V, LAST, 1)
+    evac(V, LAST, 0)
     pack(0)
-    V.wait_ge(S.mcw, 1)
-    V.tensor_scalar(T.cw[:, 0:8], T.nb[:], -1.0, None, O.mult).then_inc(S.cneg, 1)
+    evac(V, LAST, 1)
     V.wait_ge(S.cneg, 1)
-    V.wait_ge(S.wx, 1)
+    V.wait_ge(S.wx, 2)
     V.transpose(T.cwt[:], T.cw[:]).then_inc(S.cwt, 1)
     for h in HS:
         V.wait_ge(sem("al", 0, h), 1)
         V.tensor_scalar(part(T.acc, h), T["bank%d" % (albank[0] + h)][:, 0:RW], wcol(r, h), None, O.mult).then_inc(sem("ev", 0, h), 1)
-    for s in (1, 2, LAST):
-        if s == 2:
-            for h in HS:
-                weigh(V, 2, h)
-        for h in HS:
-            a = part(T.acc, h)
-            if s == LAST:
-                V.wait_ge(sem("ad", 2, h), 1)
-                V.wait_ge(sem("rl", h), arrived(diag))
-                V.tensor_scalar(T.rd[:, 4 * h:4 * h + 1], land(diag, h)[:, 128:129], wcol(diag, h), T.acc[:, RW * h + 128:RW * h + 129], O.mult, O.add).then_inc(sem("dn", h), 1)
-                V.wait_ge(sem("dn", h), 1)
-                V.reciprocal(T.rd[:, 8 + 4 * h:9 + 4 * h], T.rd[:, 4 * h:4 * h + 1]).then_inc(sem("rc", h), 1)
-                a = a[:, 0:128]
-            V.wait_ge(sem("tm", s, h), 1)
-            V.wait_ge(sem("ev", 0, h) if s == 1 else sem("ad", s - 1, h), 1)
-            V.tensor_tensor(a, a, part(T["tm%d" % s], h)[:, 0:128] if s == LAST else part(T["tm%d" % s], h), O.add).then_inc(sem("ad", s, h), 1)
+
+    def add(s, h, w=RW):
+        a = T.acc[:, RW * h:RW * h + w]
+        V.wait_ge(sem("tm", s, h), 1)
+        V.wait_ge(sem("ev", 0, h) if s == 1 else sem("ad", s - 1, h), 1)
+        V.tensor_tensor(a, a, T["tm%d" % s][:, RW * h:RW * h + w], O.add).then_inc(sem("ad", s, h), 1)
+
+    for h in HS:
+        add(1, h)
+    weigh(V, 2, 1)
+    for h in HS:
+        add(2, h)
+    for h in HS:
+        V.wait_ge(sem("ad", 2, h), 1)
+        V.wait_ge(sem("rl", h), arrived(diag))
+        V.tensor_scalar(T.rd[:, h:h + 1], land(diag, h)[:, 128:129], wcol(diag, h), T.acc[:, RW * h + 128:RW * h + 129], O.mult, O.add).then_inc(S.dn, 1)
+        if h == 0:
+            add(LAST, 0, 128)
+    V.wait_ge(S.dn, 2)
+    V.reciprocal(T.rd[:, 8:10], T.rd[:, 0:2]).then_inc(S.rc, 1)
+    add(LAST, 1, 128)
 
     def scaled(q, h):
         q.wait_ge(sem("ad", LAST, h), 1)
-        q.wait_ge(sem("rc", h), 1)
-        out, a, f = T.on[:, 128 * h:128 * h + 128], T.acc[:, RW * h:RW * h + 128], T.rd[:, 8 + 4 * h:9 + 4 * h]
+        q.wait_ge(S.rc, 1)
+        out, a, f = T.on[:, 128 * h:128 * h + 128], T.acc[:, RW * h:RW * h + 128], T.rd[:, 8 + h:9 + h]
         (q.tensor_scalar(out, a, f, None, O.mult) if q is V else q.activation(out, a, F.Copy, scale=f)).then_inc(sem("nr", h), 1)
 
     scaled(X, 0)
@@ -310,17 +332,24 @@ def rank_program(g, core, T, topo):
             c0 = 128 * h + 32 * B
             V.transpose(T.ot[:, c0:c0 + 32], T.on[:, 128 * h + B:128 * h + 128:4]).then_inc(sem("ott", h), 1)
 
-    for s, h in pieces[:-1]:
-        exchange(Y, s, h)
+    for s in range(3):
+        exchange(Y, s)
+    exchange(Y, LAST, 0)
     exchange(Y, LAST, 1, (2, 3))
-    Y.wait_ge(sem("ev", LAST, 0), 1)
-    for s in (1, 2, LAST, 0):
+
+    def store_p(s):
         for h in HS:
             Y.wait_ge(sem("cl", s, h), 4)
         Y.dma_start(T.p[rk[s]], T["p%d" % s][:]).then_inc(S.stp, 16)
+
+    Y.wait_ge(sem("ev", LAST, 0), 1)
+    store_p(1)
+    store_p(2)
     Y.wait_ge(S.cwt, 1)
     for a in range(4):
         Y.dma_start(T.cwd[:, a, :], T.cwt[32 * a:32 * a + 32, :]).then_inc(S.cwd, 16)
+    store_p(LAST)
+    store_p(0)
     Y.wait_ge(S.cwd, 64)
     Y.dma_start(T.c[:, :], T.cwd[0:8, :, :]).then_inc(S.stp, 16)
     Y.dma_start(T.w[:, :], T.cwd[8:16, :, :]).then_inc(S.stp, 16)

@@ -5,11 +5,22 @@ N = 4
 NC = 256
 A = 0.0125
 RW = 132
+LAST = 3
+BIG = 1e29
+
+VO = """one qq.0 qq.1 qk.0 qk.1 scan.0.0 scan.0.1 n.0.0 n.0.1 floor.0 floor.1 turn.0.0 turn.0.1 scan.1.0 scan.1.1 n.1.0 n.1.1 red.2.0 red.2.1
+ n.2.0 n.2.1 turn.1 red.3.0 n.3.0 turn.2 red.3.1 n.3.1 turn.3.0 qv turn.3.1 cl.1.0 cl.1.1 pack.1 cl.2.0 cl.2.1 pack.2 cl.3.0 pack.3.0 mm
+ cl.3.1 pack.3.1 pack.0 tcw own.0 own.1 add.1.0 add.1.1 add.2.0 add.2.1 den.0 rec.0 add.3.0 den.1 rec.1 to.0 add.3.1 sc.1 to.1"""
+XO = """ek half.0.0 half.0.1 exp.0.0 exp.0.1 half.1.0 half.1.1 exp.1.0 exp.1.1 exp.2.0 exp.2.1 exp.3.0 exp.3.1 ex.3.1.0.1 cown
+ weave.0 ev.1.0 ev.1.1 weave.1 ev.2.0 ev.2.1 ev.3.0 ev.3.1 wexp wt.1.0 wt.1.1 wt.2.0 wt.2.1 wt.3.0 sc.0 wt.3.1"""
+YO = """ex.0 ex.1 ex.2 ex.3.0 ex.3.1.2.3 p.1 wev.3.1 p.2 p.0 cwd p.3 cw"""
+HOME = ((1, 0, 2), (2, 0, 2), (LAST, 0, 1), (LAST, 1, 2))
 
 SCRATCH = {
     "qt": ("sbuf", [128, 1024], "bfloat16"),
     "kt": ("sbuf", [128, 2048], "bfloat16"),
-    "vt": ("sbuf", [128, 512], "bfloat16"),
+    "vt": ("sbuf", [128, 32, 4, 4], "bfloat16"),
+    "vp": ("sbuf", [128, 512], "bfloat16"),
     "one": ("sbuf", [128, 512], "bfloat16"),
     "kc": ("sbuf", [128, 8], "float32"),
     "ek": ("sbuf", [128, 8], "bfloat16"),
@@ -19,41 +30,44 @@ SCRATCH = {
     "ksc": ("sbuf", [128, 512], "uint8"),
     "vc": ("sbuf", [128, 256], "float8_e4m3fn_x4"),
     "vs": ("sbuf", [128, 256], "uint8"),
-    "nm": ("sbuf", [128, 8], "float32"),
+    "pc": ("sbuf", [128, 1024], "float8_e4m3fn_x4"),
+    "ps": ("sbuf", [128, 1024], "uint8"),
     "nb": ("sbuf", [128, 8], "float32"),
     "nbl": ("sbuf", [128, 32], "float32"),
     "mm": ("sbuf", [128, 8], "float32"),
     "cw": ("sbuf", [128, 32], "float32"),
     "cwt": ("sbuf", [128, 32], "float32"),
     "cwd": ("dram", [32, 4, 32], "float32"),
+    "res": ("sbuf", [128, 4 * 2 * RW], "float32"),
     "land": ("sbuf", [128, 4 * 2 * RW], "float32"),
+    "tm": ("sbuf", [128, 4 * 2 * RW], "float32"),
     "acc": ("sbuf", [128, 2 * RW], "float32"),
     "rd": ("sbuf", [128, 16], "float32"),
     "on": ("sbuf", [128, 256], "float32"),
     "ot": ("sbuf", [128, 256], "float32"),
+    "hs": ("sbuf", [128, 8, 256], "float32"),
+    "sc": ("sbuf", [128, 8, 256], "float32"),
 }
 for _s in range(4):
     SCRATCH["e%d" % _s] = ("sbuf", [128, 1024], "bfloat16")
     SCRATCH["i%d" % _s] = ("sbuf", [128, 1024], "bfloat16")
     SCRATCH["x%d" % _s] = ("sbuf", [128, 4, 8, 32], "bfloat16")
     SCRATCH["p%d" % _s] = ("sbuf", [128, 1024], "bfloat16")
-    SCRATCH["pc%d" % _s] = ("sbuf", [128, 256], "float8_e4m3fn_x4")
-    SCRATCH["ps%d" % _s] = ("sbuf", [128, 256], "uint8")
-    if _s:
-        SCRATCH["r%d" % _s] = ("sbuf", [128, 2 * RW], "float32")
-        SCRATCH["tm%d" % _s] = ("sbuf", [128, 2 * RW], "float32")
 for _b in range(8):
     SCRATCH["bank%d" % _b] = ("psum", [128, 512], "float32")
 
-SEMAPHORES = ["lq", "lv", "m1", "mk", "mcw", "ek", "qq", "vq", "oq", "sent", "ca", "cneg", "cown",
-              "mm", "wx", "cwt", "cwd", "sto", "stp", "dn", "rc"]
-SEMAPHORES += ["%s%d" % (a, b) for a in ("lk", "kq") for b in range(2)]
-for _s in range(4):
-    SEMAPHORES += ["%s%d" % (a, _s) for a in ("qa", "ra")]
-    for _h in range(2):
-        SEMAPHORES += ["%s%d%d" % (a, _s, _h) for a in ("st", "rm", "nb", "ex", "tr", "xd", "cl", "qz", "al", "ev", "tm", "ad")]
+SEMAPHORES = ["m1", "mk", "mcw", "ek", "vp", "lv", "vq", "oq", "sent", "ca", "cneg", "cown", "mm", "wx", "cwt", "cwd", "sto", "stp"]
 for _h in range(2):
-    SEMAPHORES += ["%s%d" % (a, _h) for a in ("rl", "nr", "ott")]
+    SEMAPHORES += ["%s%d" % (a, _h) for a in ("lq", "lk", "kq", "qq", "nr", "ott", "dn", "rc", "fl")]
+for _s in range(4):
+    for _h in range(2):
+        SEMAPHORES += ["%s%d%d" % (a, _s, _h) for a in ("qa", "ra", "st", "rm", "nb", "ex", "cl", "al", "ev")]
+        if _s:
+            SEMAPHORES += ["%s%d%d" % (a, _s, _h) for a in ("tm", "ad")]
+        if _h == 0 or _s == LAST:
+            SEMAPHORES += ["%s%d%d" % (a, _s, _h) for a in ("tr", "xd", "qz")]
+        if "half.%d.%d" % (_s, _h) in XO:
+            SEMAPHORES += ["cp%d%d" % (_s, _h)]
 
 
 def bits(mask):
@@ -79,289 +93,296 @@ def rank_program(g, core, T, topo):
     mate = [i for i in far if topo.die(T.cores[i]) == topo.die(core)][0]
     diag = [i for i in far if i != mate][0]
     rk = [r, near, mate, diag]
-    LAST = 3
     addr = {i: topo.addr(T.cores[i]) for i in others}
     off = bits(topo.mask(core, T.cores[mate]) & topo.mask(core, T.cores[diag]))
     on = bits(topo.mask(core, T.cores[near]))
     half = len(off) // 2
     inner = [b for b in on if b not in off]
-    qeng = {near: inner, mate: off, diag: off}
+    wide = {near: inner, mate: off, diag: off}
+    full = {near: on, mate: off, diag: off}
     eng = {near: inner, mate: off[:half], diag: off[half:]}
     sent = [0]
 
     def sem(a, *k):
         return S[a + "".join(str(x) for x in k)]
 
-    def shifted(s, h):
-        return sem("nb", s, 0 if s in (1, 2) else h)
-
     def tr(i, src, dst, rs, es):
         sent[0] += len(es[i])
         return RemoteDMATransfer(dst_ids=[DstId(rid=addr[i][0], pnc=addr[i][1])], dma_engine_mask=to_mask(es[i]), remote_sem=rs, src=src, dst=dst)
 
-    for buf, src, c0, w, s_ in ((T.qt, T.q, 0, 512, S.lq), (T.kt, T.k, 0, 512, S.lk0), (T.kt, T.k, 1024, 512, S.lk1), (T.vt, T.v, 0, 256, S.lv)):
-        for n, q in enumerate((Y, X)):
-            cs = slice(c0 + w * n, c0 + w * n + w)
-            q.dma_start(buf[:, cs], src[:, cs]).then_inc(s_, 16)
+    for n in HS:
+        Y.dma_start(T.qt[:, 512 * n:512 * n + 512], T.q[:, 512 * n:512 * n + 512]).then_inc(sem("lq", n), 16)
+    for n in HS:
+        Y.dma_start(T.kt[:, 1024 * n:1024 * n + 1024], T.k[:, 1024 * n:1024 * n + 1024]).then_inc(sem("lk", n), 16)
+    Y.dma_start(T.vt[:, :, :, :], T.v[:, :]).then_inc(S.lv, 16)
 
-    sl = slice(NC * r, NC * r + NC)
-    g.wait_ge(S.qq, 1)
-    for to in ((near, mate), (diag,)):
-        g.remote_dma_fused([tr(i, T.qc[:, sl].bitcast(dt.uint8), T.qc[:, sl].bitcast(dt.uint8), sem("qa", r), qeng) for i in to], local_sem=S.sent)
-        g.remote_dma_fused([tr(i, T.qs[:, sl], T.qs[:, sl], sem("qa", r), qeng) for i in to], local_sem=S.sent)
+    def qsl(i, h):
+        return slice(NC * i + 128 * h, NC * i + 128 * h + 128)
+
+    def slot(b, n, h0, h1):
+        return b[:, RW * (2 * n + h0):RW * (2 * n + h1)]
+
+    def codes(to, sl, h):
+        v = T.qc[:, sl].bitcast(dt.uint8)
+        g.remote_dma_fused([tr(i, v, v, sem("qa", r, h), wide) for i in to], local_sem=S.sent)
+
+    whole = slice(NC * r, NC * r + NC)
+    g.wait_ge(S.qq0, 1)
+    codes((near, mate), qsl(r, 0), 0)
+    g.wait_ge(S.qq1, 1)
+    g.remote_dma_fused([tr(i, T.qs[:, whole], T.qs[:, whole], sem("qa", r, 0), eng) for i in (near, mate, diag)], local_sem=S.sent)
+    codes((near, mate), qsl(r, 1), 1)
+    codes((diag,), whole, 0)
+    g.wait_ge(S.lv, 16)
+    for B in range(4):
+        g.affine_select(T.vp[:, 128 * B:128 * B + 128], T.vt[:, :, B, :], [[0, 32], [0, 4]], O.is_ge, 0.0, 0, 0).then_inc(S.vp, 1)
     for s in range(4):
         for h in HS:
-            g.wait_ge(shifted(s, h), 1)
+            g.wait_ge(sem("nb", s, h), 1)
     g.remote_dma_fused([tr(i, T.nb[:], T.nbl[:, 8 * r:8 * r + 8], S.ca, eng) for i in (near, mate, diag)], local_sem=S.sent)
-
-    def home(s, c0, c1, rs):
-        i = rk[s]
-        m = bits(topo.mask(core, T.cores[i]))
-        g.remote_dma(T["land"][:, 2 * RW * r + c0:2 * RW * r + c1], T["r%d" % s][:, c0:c1], rs, S.sent, addr[i][1], addr[i][0], to_mask(m))
-        sent[0] += len(m)
-
-    for s in (1, 2):
-        for h in HS:
+    for s, h0, h1 in HOME:
+        for h in range(h0, h1):
             g.wait_ge(sem("ev", s, h), 1)
-        home(s, 0, 2 * RW, sem("ra", r))
-    for h in HS:
-        g.wait_ge(sem("ev", LAST, h), 1)
-        home(LAST, RW * h, RW * h + RW, sem("rl", h))
+        g.remote_dma_fused([tr(rk[s], slot(T.res, s, h0, h1), slot(T["land"], r, h0, h1), sem("ra", r, h0), full)], local_sem=S.sent)
     g.wait_ge(S.sent, sent[0])
 
-    for s in range(4):
-        i = rk[s]
-        if s == 0:
-            P.wait_ge(S.qq, 1)
-            P.wait_ge(S.kq0, 1)
-            P.wait_ge(S.kq1, 1)
-        else:
-            P.wait_ge(sem("qa", i), 2 * len(qeng[i]))
+    def scores(b, i, h, c0, c1, s):
+        P.matmul_mx(T["bank%d" % b][:, 0:c1 - c0], T.qc[:, qsl(i, h)], T.qs[:, qsl(i, h)], T.kcd[:, c0:c1], T.ksc[:, c0:c1], True, True).then_inc(sem("st", s, h), 1)
+
+    for n in HS:
+        P.wait_ge(sem("kq", n), 1)
         for h in HS:
-            c0 = NC * i + 128 * h
-            P.matmul_mx(T["bank%d" % (2 * s + h)][:], T.qc[:, c0:c0 + 128], T.qs[:, c0:c0 + 128], T.kcd[:], T.ksc[:], True, True).then_inc(sem("st", s, h), 1)
+            if n == 0:
+                P.wait_ge(sem("qq", h), 1)
+            scores(2 * h + n, r, h, 256 * n, 256 * n + 256, 0)
+    bank = {1: (4, 5), 2: (6, 7), LAST: (0, 1)}
+    for s in (1, 2, LAST):
+        i = rk[s]
+        for h in HS:
+            if h == 0:
+                P.wait_ge(sem("qa", i, 0), len(wide[i]) + len(eng[i]))
+            elif s != LAST:
+                P.wait_ge(sem("qa", i, 1), len(wide[i]))
+            if s == LAST and h == 0:
+                P.wait_ge(sem("ex", 0, 0), 2)
+            scores(bank[s][h], i, h, 0, 512, s)
     P.wait_ge(S.vq, 1)
     P.wait_ge(S.oq, 1)
-    albank = {1: 0, 2: 2, LAST: 4, 0: 6}
+    albank = {1: (2, 3), 2: (4, 5), LAST: (6, 7), 0: (0, 1)}
+    was = {2: 1, LAST: 2, 0: LAST}
     for s in (1, 2, LAST, 0):
         for h in HS:
-            b = albank[s] + h
             P.wait_ge(sem("qz", s, h if s == LAST else 0), 1)
-            P.wait_ge(sem("ex", b // 2, b % 2), 1)
-            P.matmul_mx(T["bank%d" % b][:, 0:256], T["pc%d" % s][:, 128 * h:128 * h + 128], T["ps%d" % s][:, 128 * h:128 * h + 128],
-                        T.vc[:], T.vs[:], True, True).then_inc(sem("al", s, h), 1)
+            if s == 1:
+                P.wait_ge(sem("ex", 0, 1), 2)
+            else:
+                P.wait_ge(sem("ex", was[s], h), 1)
+            P.matmul_mx(T["bank%d" % albank[s][h]][:, 0:256], T.pc[:, qsl(s, h)], T.ps[:, qsl(s, h)], T.vc[:], T.vs[:], True, True).then_inc(sem("al", s, h), 1)
 
-    X.wait_ge(S.mk, 1)
-    X.activation(T.ek[:, 0:1], T.kc[:, 0:1], F.Exp).then_inc(S.ek, 1)
-    for s in range(4):
-        for h in HS:
-            col = 2 * rk[s] + h
-            X.wait_ge(shifted(s, h), 1)
-            X.activation(T["e%d" % s][:, 512 * h:512 * h + 512], T["bank%d" % (2 * s + h)][:], F.Exp, bias=T.nb[:, col:col + 1], scale=A).then_inc(sem("ex", s, h), 1)
+    def scored(s, h, n):
+        return T["bank%d" % (2 * h + n)][:, 0:256] if s == 0 else T["bank%d" % bank[s][h]][:, 256 * n:256 * n + 256]
 
-    def exchange(q, s, h=0, quads=range(4)):
+    def half_out(q, s, h):
+        q.wait_ge(sem("st", s, h), 1)
+        q.activation(T.hs[:, 2 * s + h, :], scored(s, h, 0), F.Copy).then_inc(sem("cp", s, h), 1)
+
+    def scan(q, s, h):
+        q.wait_ge(sem("st", s, h), 1 if s else 2)
+        q.wait_ge(sem("cp", s, h), 1)
+        q.tensor_tensor_scan(T.sc[:, 2 * s + h, :], scored(s, h, 1), T.hs[:, 2 * s + h, :], -BIG, O.max, O.max).then_inc(sem("rm", s, h), 1)
+
+    def red(q, s, h):
+        q.wait_ge(sem("st", s, h), 1)
+        q.tensor_reduce(T.sc[:, 2 * s + h, 255:256], T["bank%d" % bank[s][h]][:], AxisListType.X, O.max).then_inc(sem("rm", s, h), 1)
+
+    def times(q, out, a, f):
+        return q.tensor_scalar(out, a, f, None, O.mult) if q is V else q.activation(out, a, F.Copy, scale=f)
+
+    def neg(q, s, h):
+        q.wait_ge(sem("rm", s, h), 1)
+        col = 2 * rk[s] + h
+        times(q, T.nb[:, col:col + 1], T.sc[:, 2 * s + h, 255:256], -A).then_inc(sem("nb", s, h), 1)
+
+    def expo(q, s, h):
+        col = 2 * rk[s] + h
+        q.wait_ge(sem("nb", s, h), 1)
+        for c0, w, src in ((0, 256, scored(0, h, 0)), (256, 256, scored(0, h, 1))) if s == 0 else ((0, 512, T["bank%d" % bank[s][h]][:]),):
+            c0 += 512 * h
+            q.activation(T["e%d" % s][:, c0:c0 + w], src, F.Exp, bias=T.nb[:, col:col + 1], scale=A).then_inc(sem("ex", s, h), 1)
+
+    def floor0(q, h):
+        q.wait_ge(sem("ex", 0, h), 2)
+        q.wait_ge(S.ek, 1)
+        a = T.e0[:, 512 * h:512 * h + 512]
+        q.tensor_scalar(a, a, T.ek[:, 0:1], None, O.max).then_inc(sem("fl", h), 1)
+
+    def turn(q, s, *hs):
+        hs = hs or HS
+        for h in hs:
+            q.wait_ge(sem("ex", s, h) if s else sem("fl", h), 1)
+        w = 128 * len(hs)
+        for B in range(4):
+            c0 = 512 * hs[0]
+            d0 = 256 * B + 128 * hs[0] if s == 0 else c0 + w * B
+            q.transpose(T["i%d" % s][:, d0:d0 + w], T["e%d" % s][:, c0 + B:c0 + 4 * w:4]).then_inc(sem("tr", s, hs[0] if s else 0), 1)
+
+    def exchange(q, s, h=0, *quads):
         q.wait_ge(sem("tr", s, h), 4 if s else 8)
-        for tq in quads:
+        for tq in quads or range(4):
             rows = slice(32 * tq, 32 * tq + 32)
             if s == LAST:
                 q.dma_start(T["x%d" % s][:, tq, 4 * h:4 * h + 4, :], T["i%d" % s][rows, 512 * h:512 * h + 512]).then_inc(sem("xd", s, h), 16)
             else:
                 q.dma_start(T["x%d" % s][:, tq, :, :], T["i%d" % s][rows, :]).then_inc(sem("xd", s, 0), 16)
 
-    exchange(X, LAST, 1, (0, 1))
-    X.wait_ge(S.mcw, 1)
-    X.activation(T.cw[:, 0:8], T.nb[:], F.Copy, scale=-1.0).then_inc(S.cneg, 1)
+    def clamp(q, s, h):
+        q.wait_ge(sem("xd", s, h if s == LAST else 0), 64)
+        if q is V:
+            q.wait_ge(S.ek, 1)
+        for b in range(4):
+            out, src = T["p%d" % s][:, 512 * h + b:512 * h + 512:4], T["x%d" % s][:, :, 4 * h + b, :]
+            (q.tensor_scalar(out, src, T.ek[:, 0:1], None, O.max) if q is V else q.activation(out, src, F.Copy)).then_inc(sem("cl", s, h), 1)
 
-    def part(b, h):
-        return b[:, RW * h:RW * h + RW]
+    def weave(q, h):
+        clamp(q, 0, h)
 
-    def evac(q, s, h):
-        q.wait_ge(sem("al", s, h), 1)
-        src = T["bank%d" % (albank[s] + h)][:, 0:RW]
-        out = part(T["r%d" % s], h)
-        (q.tensor_copy(out, src) if q is V else q.activation(out, src, F.Copy)).then_inc(sem("ev", s, h), 1)
+    def pack(q, s, *hs):
+        hs = hs or HS
+        for h in hs:
+            q.wait_ge(sem("cl", s, h), 4)
+        a, b = 128 * hs[0], 128 * hs[-1] + 128
+        d = slice(NC * s + a, NC * s + b)
+        q.quantize_mx(T.pc[:, d], T.ps[:, d], T["p%d" % s][:, 4 * a:4 * b]).then_inc(sem("qz", s, hs[0]), 1)
 
-    def land(j, h):
-        return T["land"][:, 2 * RW * j + RW * h:2 * RW * j + RW * h + RW]
+    def ekc(q):
+        q.wait_ge(S.mk, 1)
+        q.activation(T.ek[:, 0:1], T.kc[:, 0:1], F.Exp).then_inc(S.ek, 1)
+
+    def own_c(q):
+        for s in range(4):
+            for h in HS:
+                q.wait_ge(sem("nb", s, h), 1)
+        q.activation(T.nbl[:, 8 * r:8 * r + 8], T.nb[:], F.Copy).then_inc(S.cown, 1)
+        q.wait_ge(S.mcw, 1)
+        q.activation(T.cw[:, 0:8], T.nb[:], F.Copy, scale=-1.0).then_inc(S.cneg, 1)
+
+    def mmax(q):
+        q.wait_ge(S.ca, sum(len(eng[i]) for i in others))
+        q.wait_ge(S.cown, 1)
+        for h in HS:
+            q.tensor_reduce(T.mm[:, h:h + 1], T.nbl[:, 2 * r + h:32:8], AxisListType.X, O.min).then_inc(S.mm, 1)
+
+    def wexp(q):
+        q.wait_ge(S.mm, 2)
+        for h in HS:
+            q.activation(T.cw[:, 8 + h:16:2], T.nbl[:, 2 * r + h:32:8], F.Exp, bias=T.mm[:, h:h + 1], scale=-1.0).then_inc(S.wx, 1)
+        q.wait_ge(S.wx, 2)
+
+    def turn_cw(q):
+        q.wait_ge(S.cneg, 1)
+        q.wait_ge(S.wx, 2)
+        q.transpose(T.cwt[:], T.cw[:]).then_inc(S.cwt, 1)
+
+    def part(b, n, h):
+        return slot(b, n, h, h + 1)
 
     def wcol(j, h):
         return T.cw[:, 8 + 2 * j + h:9 + 2 * j + h]
 
-    arrived = lambda i: len(bits(topo.mask(core, T.cores[i])))
+    def arrived(q, s, h):
+        q.wait_ge(sem("ra", rk[s], h if s == LAST else 0), len(full[rk[s]]))
+
+    def evac(q, s, h):
+        q.wait_ge(sem("al", s, h), 1)
+        q.activation(part(T.res, s, h), T["bank%d" % albank[s][h]][:, 0:RW], F.Copy).then_inc(sem("ev", s, h), 1)
 
     def weigh(q, s, h):
-        i = rk[s]
-        q.wait_ge(sem("rl", h) if s == LAST else sem("ra", i), arrived(i))
-        out = part(T["tm%d" % s], h)
-        (q.tensor_scalar(out, land(i, h), wcol(i, h), None, O.mult) if q is V else
-         q.activation(out, land(i, h), F.Copy, scale=wcol(i, h))).then_inc(sem("tm", s, h), 1)
+        arrived(q, s, h)
+        times(q, part(T.tm, s, h), part(T["land"], rk[s], h), wcol(rk[s], h)).then_inc(sem("tm", s, h), 1)
 
-    for s in (1, 2):
-        for h in HS:
-            evac(X, s, h)
-    X.wait_ge(S.mm, 2)
-    for h in HS:
-        X.activation(T.cw[:, 8 + h:16:2], T.nbl[:, 2 * r + h:32:8], F.Exp, bias=T.mm[:, h:h + 1], scale=-1.0).then_inc(S.wx, 1)
-    X.wait_ge(S.wx, 2)
-    for s in (1, 2, LAST):
-        for h in HS:
-            if (s, h) != (2, 1):
-                weigh(X, s, h)
+    def own(q, h):
+        q.wait_ge(sem("al", 0, h), 1)
+        q.wait_ge(S.wx, 2)
+        times(q, part(T.acc, 0, h), T["bank%d" % albank[0][h]][:, 0:RW], wcol(r, h)).then_inc(sem("ev", 0, h), 1)
 
-    V.memset(T.one[:], 1.0).then_inc(S.m1, 1)
-    V.memset(T.kc[:], -20.0).then_inc(S.mk, 1)
-    V.memset(T.cw[:], 0.0).then_inc(S.mcw, 1)
-    V.wait_ge(S.m1, 1)
-    V.quantize_mx(T.vc[:, 128:256], T.vs[:, 128:256], T.one[:]).then_inc(S.oq, 1)
-    V.wait_ge(S.lq, 32)
-    V.quantize_mx(T.qc[:, sl], T.qs[:, sl], T.qt[:]).then_inc(S.qq, 1)
-    for n in range(2):
-        V.wait_ge(sem("lk", n), 32)
-        V.quantize_mx(T.kcd[:, 256 * n:256 * n + 256], T.ksc[:, 256 * n:256 * n + 256], T.kt[:, 1024 * n:1024 * n + 1024]).then_inc(sem("kq", n), 1)
+    def add(q, s, h):
+        w = 128 if s == LAST else RW
+        a = part(T.acc, 0, h)[:, 0:w]
+        q.wait_ge(sem("tm", s, h), 1)
+        q.wait_ge(sem("ev", 0, h) if s == 1 else sem("ad", s - 1, h), 1)
+        q.tensor_tensor(a, a, part(T.tm, s, h)[:, 0:w], O.add).then_inc(sem("ad", s, h), 1)
 
-    def shift(s, *hs):
-        col = 2 * rk[s] + hs[0]
-        for n, h in enumerate(hs):
-            V.wait_ge(sem("st", s, h), 1)
-            V.tensor_reduce(T.nm[:, col + n:col + n + 1], T["bank%d" % (2 * s + h)][:], AxisListType.X, O.max, negate=True).then_inc(sem("rm", s, h), 1)
-        for h in hs:
-            V.wait_ge(sem("rm", s, h), 1)
-        V.tensor_scalar(T.nb[:, col:col + len(hs)], T.nm[:, col:col + len(hs)], A, None, O.mult).then_inc(shifted(s, hs[0]), 1)
+    def den(q, h):
+        q.wait_ge(sem("ad", 2, h), 1)
+        arrived(q, LAST, h)
+        q.tensor_scalar(T.rd[:, h:h + 1], part(T["land"], diag, h)[:, 128:129], wcol(diag, h), part(T.acc, 0, h)[:, 128:129], O.mult, O.add).then_inc(sem("dn", h), 1)
 
-    def turn(s, hs=HS):
-        for h in hs:
-            V.wait_ge(sem("ex", s, h), 1)
-        w = 128 * len(hs)
-        for B in range(4):
-            c0 = 512 * hs[0]
-            V.transpose(T["i%d" % s][:, c0 + w * B:c0 + w * B + w], T["e%d" % s][:, c0 + B:c0 + 4 * w:4]).then_inc(sem("tr", s, hs[0]), 1)
-
-    def turn_own(h):
-        V.wait_ge(sem("ex", 0, h), 1)
-        for B in range(4):
-            V.transpose(T.i0[:, 256 * B + 128 * h:256 * B + 128 * h + 128], T.e0[:, 512 * h + B:512 * h + 512:4]).then_inc(sem("tr", 0, 0), 1)
-
-    def clamp(s, h):
-        V.wait_ge(sem("xd", s, h if s == LAST else 0), 64)
-        for b in range(4):
-            V.tensor_scalar(T["p%d" % s][:, 512 * h + b:512 * h + 512:4], T["x%d" % s][:, :, 4 * h + b, :], T.ek[:, 0:1], None, O.max).then_inc(sem("cl", s, h), 1)
-
-    def pack(s, hs=HS):
-        for h in hs:
-            V.wait_ge(sem("cl", s, h), 4)
-        a, b = 128 * hs[0], 128 * hs[-1] + 128
-        V.quantize_mx(T["pc%d" % s][:, a:b], T["ps%d" % s][:, a:b], T["p%d" % s][:, 4 * a:4 * b]).then_inc(sem("qz", s, hs[0]), 1)
-
-    shift(0, 0)
-    shift(0, 1)
-    V.wait_ge(S.lv, 32)
-    V.quantize_mx(T.vc[:, 0:128], T.vs[:, 0:128], T.vt[:]).then_inc(S.vq, 1)
-    turn_own(0)
-    shift(1, 0, 1)
-    turn_own(1)
-    shift(2, 0, 1)
-    turn(1)
-    shift(LAST, 0)
-    turn(2)
-    shift(LAST, 1)
-    turn(LAST, (0,))
-    V.wait_ge(S.ek, 1)
-    clamp(0, 0)
-    turn(LAST, (1,))
-    for h in HS:
-        clamp(1, h)
-    pack(1)
-    clamp(0, 1)
-    for h in HS:
-        clamp(2, h)
-    pack(2)
-    clamp(LAST, 0)
-    pack(LAST, (0,))
-    for s in range(4):
-        for h in HS:
-            V.wait_ge(shifted(s, h), 1)
-    V.tensor_copy(T.nbl[:, 8 * r:8 * r + 8], T.nb[:]).then_inc(S.cown, 1)
-    V.wait_ge(S.ca, sum(len(eng[i]) for i in others))
-    V.wait_ge(S.cown, 1)
-    for h in HS:
-        V.tensor_reduce(T.mm[:, h:h + 1], T.nbl[:, 2 * r + h:32:8], AxisListType.X, O.min).then_inc(S.mm, 1)
-    clamp(LAST, 1)
-    pack(LAST, (1,))
-    evac(V, LAST, 0)
-    pack(0)
-    evac(V, LAST, 1)
-    V.wait_ge(S.cneg, 1)
-    V.wait_ge(S.wx, 2)
-    V.transpose(T.cwt[:], T.cw[:]).then_inc(S.cwt, 1)
-    for h in HS:
-        V.wait_ge(sem("al", 0, h), 1)
-        V.tensor_scalar(part(T.acc, h), T["bank%d" % (albank[0] + h)][:, 0:RW], wcol(r, h), None, O.mult).then_inc(sem("ev", 0, h), 1)
-
-    def add(s, h, w=RW):
-        a = T.acc[:, RW * h:RW * h + w]
-        V.wait_ge(sem("tm", s, h), 1)
-        V.wait_ge(sem("ev", 0, h) if s == 1 else sem("ad", s - 1, h), 1)
-        V.tensor_tensor(a, a, T["tm%d" % s][:, RW * h:RW * h + w], O.add).then_inc(sem("ad", s, h), 1)
-
-    for h in HS:
-        add(1, h)
-    weigh(V, 2, 1)
-    for h in HS:
-        add(2, h)
-    for h in HS:
-        V.wait_ge(sem("ad", 2, h), 1)
-        V.wait_ge(sem("rl", h), arrived(diag))
-        V.tensor_scalar(T.rd[:, h:h + 1], land(diag, h)[:, 128:129], wcol(diag, h), T.acc[:, RW * h + 128:RW * h + 129], O.mult, O.add).then_inc(S.dn, 1)
-        if h == 0:
-            add(LAST, 0, 128)
-    V.wait_ge(S.dn, 2)
-    V.reciprocal(T.rd[:, 8:10], T.rd[:, 0:2]).then_inc(S.rc, 1)
-    add(LAST, 1, 128)
+    def rec(q, h):
+        q.wait_ge(sem("dn", h), 1)
+        q.reciprocal(T.rd[:, 8 + h:9 + h], T.rd[:, h:h + 1]).then_inc(sem("rc", h), 1)
 
     def scaled(q, h):
         q.wait_ge(sem("ad", LAST, h), 1)
-        q.wait_ge(S.rc, 1)
-        out, a, f = T.on[:, 128 * h:128 * h + 128], T.acc[:, RW * h:RW * h + 128], T.rd[:, 8 + h:9 + h]
-        (q.tensor_scalar(out, a, f, None, O.mult) if q is V else q.activation(out, a, F.Copy, scale=f)).then_inc(sem("nr", h), 1)
+        q.wait_ge(sem("rc", h), 1)
+        times(q, T.on[:, 128 * h:128 * h + 128], part(T.acc, 0, h)[:, 0:128], T.rd[:, 8 + h:9 + h]).then_inc(sem("nr", h), 1)
 
-    scaled(X, 0)
-    scaled(V, 1)
-    for h in HS:
-        V.wait_ge(sem("nr", h), 1)
-        for B in range(4):
-            c0 = 128 * h + 32 * B
-            V.transpose(T.ot[:, c0:c0 + 32], T.on[:, 128 * h + B:128 * h + 128:4]).then_inc(sem("ott", h), 1)
+    def turn_o(q, h):
+        q.wait_ge(sem("nr", h), 1)
+        q.transpose(T.ot[:, 128 * h:128 * h + 128], T.on[:, 128 * h:128 * h + 128]).then_inc(sem("ott", h), 1)
 
-    for s in range(3):
-        exchange(Y, s)
-    exchange(Y, LAST, 0)
-    exchange(Y, LAST, 1, (2, 3))
+    def consts(q):
+        q.memset(T.one[:], 1.0).then_inc(S.m1, 1)
+        q.memset(T.kc[:], -20.0).then_inc(S.mk, 1)
+        q.memset(T.cw[:], 0.0).then_inc(S.mcw, 1)
+        q.wait_ge(S.m1, 1)
+        q.quantize_mx(T.vc[:, 128:256], T.vs[:, 128:256], T.one[:]).then_inc(S.oq, 1)
 
-    def store_p(s):
+    def pack_q(q, h):
+        q.wait_ge(sem("lq", h), 16)
+        q.quantize_mx(T.qc[:, qsl(r, h)], T.qs[:, qsl(r, h)], T.qt[:, 512 * h:512 * h + 512]).then_inc(sem("qq", h), 1)
+
+    def pack_k(q, n):
+        q.wait_ge(sem("lk", n), 16)
+        q.quantize_mx(T.kcd[:, 256 * n:256 * n + 256], T.ksc[:, 256 * n:256 * n + 256], T.kt[:, 1024 * n:1024 * n + 1024]).then_inc(sem("kq", n), 1)
+
+    def pack_v(q):
+        q.wait_ge(S.vp, 4)
+        q.quantize_mx(T.vc[:, 0:128], T.vs[:, 0:128], T.vp[:]).then_inc(S.vq, 1)
+
+    def store_p(q, s):
         for h in HS:
-            Y.wait_ge(sem("cl", s, h), 4)
-        Y.dma_start(T.p[rk[s]], T["p%d" % s][:]).then_inc(S.stp, 16)
+            q.wait_ge(sem("cl", s, h), 4)
+        q.dma_start(T.p[rk[s]], T["p%d" % s][:]).then_inc(S.stp, 16)
 
-    Y.wait_ge(sem("ev", LAST, 0), 1)
-    store_p(1)
-    store_p(2)
-    Y.wait_ge(S.cwt, 1)
-    for a in range(4):
-        Y.dma_start(T.cwd[:, a, :], T.cwt[32 * a:32 * a + 32, :]).then_inc(S.cwd, 16)
-    store_p(LAST)
-    store_p(0)
-    Y.wait_ge(S.cwd, 64)
-    Y.dma_start(T.c[:, :], T.cwd[0:8, :, :]).then_inc(S.stp, 16)
-    Y.dma_start(T.w[:, :], T.cwd[8:16, :, :]).then_inc(S.stp, 16)
+    def wait_ev(q, s, h):
+        q.wait_ge(sem("ev", s, h), 1)
+
+    def cw_dram(q):
+        q.wait_ge(S.cwt, 1)
+        for a in range(4):
+            q.dma_start(T.cwd[:, a, :], T.cwt[32 * a:32 * a + 32, :]).then_inc(S.cwd, 16)
+
+    def cw_store(q):
+        q.wait_ge(S.cwd, 64)
+        q.dma_start(T.c[:, :], T.cwd[0:8, :, :]).then_inc(S.stp, 16)
+        q.dma_start(T.w[:, :], T.cwd[8:16, :, :]).then_inc(S.stp, 16)
+
+    CALLS = {"one": consts, "qq": pack_q, "qk": pack_k, "qv": pack_v, "red": red, "scan": scan, "half": half_out, "n": neg, "exp": expo, "floor": floor0,
+             "turn": turn, "ex": exchange, "cl": clamp, "weave": weave, "pack": pack, "ek": ekc, "cown": own_c, "mm": mmax, "wexp": wexp,
+             "tcw": turn_cw, "ev": evac, "wt": weigh, "own": own, "add": add, "den": den, "rec": rec, "sc": scaled, "to": turn_o, "p": store_p,
+             "wev": wait_ev, "cwd": cw_dram, "cw": cw_store}
+    for q, order in ((V, VO), (X, XO), (Y, YO)):
+        for word in order.split():
+            n, *k = word.split(".")
+            CALLS[n](q, *[int(x) for x in k])
 
     def store_o(q, h, quads, sm):
-        q.wait_ge(sem("ott", h), 4)
+        q.wait_ge(sem("ott", h), 1)
         for tq in quads:
             q.dma_start(T.o[:, 128 * h + 32 * tq:128 * h + 32 * tq + 32], T.ot[32 * tq:32 * tq + 32, 128 * h:128 * h + 128]).then_inc(sm, 16)
 
-    store_o(Y, 0, (0, 1), S.stp)
-    store_o(X, 0, (2, 3), S.sto)
+    store_o(Y, 0, range(4), S.stp)
     store_o(Y, 1, (0, 1), S.stp)
     store_o(X, 1, (2, 3), S.sto)
-    Y.wait_ge(S.stp, 16 * 10)
-    X.wait_ge(S.sto, 16 * 4)
+    Y.wait_ge(S.stp, 16 * 12)
+    X.wait_ge(S.sto, 16 * 2)

from concourse.bass import DstId, RemoteDMATransfer
from concourse.mybir import dt, AluOpType, AxisListType, ActivationFunctionType

N = 4
NC = 256
A = 0.0125
RW = 132
LAST = 3
BIG = 1e29

VO = """one qq.0 qq.1 qk.0 qk.1 scan.0.0 scan.0.1 n.0.0 n.0.1 floor.0 floor.1 turn.0.0 turn.0.1 scan.1.0 scan.1.1 n.1.0 n.1.1 red.2.0 red.2.1
 n.2.0 n.2.1 turn.1 red.3.0 n.3.0 turn.2 red.3.1 n.3.1 turn.3.0 qv turn.3.1 cl.1.0 cl.1.1 pack.1 cl.2.0 cl.2.1 pack.2 cl.3.0 pack.3.0 mm
 cl.3.1 pack.3.1 pack.0 tcw own.0 own.1 add.1.0 add.1.1 add.2.0 add.2.1 den.0 rec.0 add.3.0 den.1 rec.1 to.0 add.3.1 sc.1 to.1"""
XO = """ek half.0.0 half.0.1 exp.0.0 exp.0.1 half.1.0 half.1.1 exp.1.0 exp.1.1 exp.2.0 exp.2.1 exp.3.0 exp.3.1 ex.3.1.0.1 cown
 weave.0 ev.1.0 ev.1.1 weave.1 ev.2.0 ev.2.1 ev.3.0 ev.3.1 wexp wt.1.0 wt.1.1 wt.2.0 wt.2.1 wt.3.0 sc.0 wt.3.1"""
YO = """ex.0 ex.1 ex.2 ex.3.0 ex.3.1.2.3 p.1 wev.3.1 p.2 p.0 cwd p.3 cw"""
HOME = ((1, 0, 2), (2, 0, 2), (LAST, 0, 1), (LAST, 1, 2))

SCRATCH = {
    "qt": ("sbuf", [128, 1024], "bfloat16"),
    "kt": ("sbuf", [128, 2048], "bfloat16"),
    "vt": ("sbuf", [128, 32, 4, 4], "bfloat16"),
    "vp": ("sbuf", [128, 512], "bfloat16"),
    "one": ("sbuf", [128, 512], "bfloat16"),
    "kc": ("sbuf", [128, 8], "float32"),
    "ek": ("sbuf", [128, 8], "bfloat16"),
    "qc": ("sbuf", [128, 1024], "float8_e4m3fn_x4"),
    "qs": ("sbuf", [128, 1024], "uint8"),
    "kcd": ("sbuf", [128, 512], "float8_e4m3fn_x4"),
    "ksc": ("sbuf", [128, 512], "uint8"),
    "vc": ("sbuf", [128, 256], "float8_e4m3fn_x4"),
    "vs": ("sbuf", [128, 256], "uint8"),
    "pc": ("sbuf", [128, 1024], "float8_e4m3fn_x4"),
    "ps": ("sbuf", [128, 1024], "uint8"),
    "nb": ("sbuf", [128, 8], "float32"),
    "nbl": ("sbuf", [128, 32], "float32"),
    "mm": ("sbuf", [128, 8], "float32"),
    "cw": ("sbuf", [128, 32], "float32"),
    "cwt": ("sbuf", [128, 32], "float32"),
    "cwd": ("dram", [32, 4, 32], "float32"),
    "res": ("sbuf", [128, 4 * 2 * RW], "float32"),
    "land": ("sbuf", [128, 4 * 2 * RW], "float32"),
    "tm": ("sbuf", [128, 4 * 2 * RW], "float32"),
    "acc": ("sbuf", [128, 2 * RW], "float32"),
    "rd": ("sbuf", [128, 16], "float32"),
    "on": ("sbuf", [128, 256], "float32"),
    "ot": ("sbuf", [128, 256], "float32"),
    "hs": ("sbuf", [128, 8, 256], "float32"),
    "sc": ("sbuf", [128, 8, 256], "float32"),
}
for _s in range(4):
    SCRATCH["e%d" % _s] = ("sbuf", [128, 1024], "bfloat16")
    SCRATCH["i%d" % _s] = ("sbuf", [128, 1024], "bfloat16")
    SCRATCH["x%d" % _s] = ("sbuf", [128, 4, 8, 32], "bfloat16")
    SCRATCH["p%d" % _s] = ("sbuf", [128, 1024], "bfloat16")
for _b in range(8):
    SCRATCH["bank%d" % _b] = ("psum", [128, 512], "float32")

SEMAPHORES = ["m1", "mk", "mcw", "ek", "vp", "lv", "vq", "oq", "sent", "ca", "cneg", "cown", "mm", "wx", "cwt", "cwd", "sto", "stp"]
for _h in range(2):
    SEMAPHORES += ["%s%d" % (a, _h) for a in ("lq", "lk", "kq", "qq", "nr", "ott", "dn", "rc", "fl")]
for _s in range(4):
    for _h in range(2):
        SEMAPHORES += ["%s%d%d" % (a, _s, _h) for a in ("qa", "ra", "st", "rm", "nb", "ex", "cl", "al", "ev")]
        if _s:
            SEMAPHORES += ["%s%d%d" % (a, _s, _h) for a in ("tm", "ad")]
        if _h == 0 or _s == LAST:
            SEMAPHORES += ["%s%d%d" % (a, _s, _h) for a in ("tr", "xd", "qz")]
        if "half.%d.%d" % (_s, _h) in XO:
            SEMAPHORES += ["cp%d%d" % (_s, _h)]


def bits(mask):
    return [b for b in range(mask.bit_length()) if mask >> b & 1]


def to_mask(bs):
    return sum(1 << b for b in bs)


def rank_program(g, core, T, topo):
    r = T.rank_of(core)
    if r is None:
        return
    S = T.sem
    F = ActivationFunctionType
    O = AluOpType
    V, X, P, Y = g.vector, g.scalar, g.tensor, g.sync
    HS = (0, 1)
    others = [i for i in range(N) if i != r]
    near = [i for i in others if topo.chip(T.cores[i]) == topo.chip(core)][0]
    far = [i for i in others if i != near]
    mate = [i for i in far if topo.die(T.cores[i]) == topo.die(core)][0]
    diag = [i for i in far if i != mate][0]
    rk = [r, near, mate, diag]
    addr = {i: topo.addr(T.cores[i]) for i in others}
    off = bits(topo.mask(core, T.cores[mate]) & topo.mask(core, T.cores[diag]))
    on = bits(topo.mask(core, T.cores[near]))
    half = len(off) // 2
    inner = [b for b in on if b not in off]
    wide = {near: inner, mate: off, diag: off}
    full = {near: on, mate: off, diag: off}
    eng = {near: inner, mate: off[:half], diag: off[half:]}
    sent = [0]

    def sem(a, *k):
        return S[a + "".join(str(x) for x in k)]

    def tr(i, src, dst, rs, es):
        sent[0] += len(es[i])
        return RemoteDMATransfer(dst_ids=[DstId(rid=addr[i][0], pnc=addr[i][1])], dma_engine_mask=to_mask(es[i]), remote_sem=rs, src=src, dst=dst)

    for n in HS:
        Y.dma_start(T.qt[:, 512 * n:512 * n + 512], T.q[:, 512 * n:512 * n + 512]).then_inc(sem("lq", n), 16)
    for n in HS:
        Y.dma_start(T.kt[:, 1024 * n:1024 * n + 1024], T.k[:, 1024 * n:1024 * n + 1024]).then_inc(sem("lk", n), 16)
    Y.dma_start(T.vt[:, :, :, :], T.v[:, :]).then_inc(S.lv, 16)

    def qsl(i, h):
        return slice(NC * i + 128 * h, NC * i + 128 * h + 128)

    def slot(b, n, h0, h1):
        return b[:, RW * (2 * n + h0):RW * (2 * n + h1)]

    def codes(to, sl, h):
        v = T.qc[:, sl].bitcast(dt.uint8)
        g.remote_dma_fused([tr(i, v, v, sem("qa", r, h), wide) for i in to], local_sem=S.sent)

    whole = slice(NC * r, NC * r + NC)
    g.wait_ge(S.qq0, 1)
    codes((near, mate), qsl(r, 0), 0)
    g.wait_ge(S.qq1, 1)
    g.remote_dma_fused([tr(i, T.qs[:, whole], T.qs[:, whole], sem("qa", r, 0), eng) for i in (near, mate, diag)], local_sem=S.sent)
    codes((near, mate), qsl(r, 1), 1)
    codes((diag,), whole, 0)
    g.wait_ge(S.lv, 16)
    for B in range(4):
        g.affine_select(T.vp[:, 128 * B:128 * B + 128], T.vt[:, :, B, :], [[0, 32], [0, 4]], O.is_ge, 0.0, 0, 0).then_inc(S.vp, 1)
    for s in range(4):
        for h in HS:
            g.wait_ge(sem("nb", s, h), 1)
    g.remote_dma_fused([tr(i, T.nb[:], T.nbl[:, 8 * r:8 * r + 8], S.ca, eng) for i in (near, mate, diag)], local_sem=S.sent)
    for s, h0, h1 in HOME:
        for h in range(h0, h1):
            g.wait_ge(sem("ev", s, h), 1)
        g.remote_dma_fused([tr(rk[s], slot(T.res, s, h0, h1), slot(T["land"], r, h0, h1), sem("ra", r, h0), full)], local_sem=S.sent)
    g.wait_ge(S.sent, sent[0])

    def scores(b, i, h, c0, c1, s):
        P.matmul_mx(T["bank%d" % b][:, 0:c1 - c0], T.qc[:, qsl(i, h)], T.qs[:, qsl(i, h)], T.kcd[:, c0:c1], T.ksc[:, c0:c1], True, True).then_inc(sem("st", s, h), 1)

    for n in HS:
        P.wait_ge(sem("kq", n), 1)
        for h in HS:
            if n == 0:
                P.wait_ge(sem("qq", h), 1)
            scores(2 * h + n, r, h, 256 * n, 256 * n + 256, 0)
    bank = {1: (4, 5), 2: (6, 7), LAST: (0, 1)}
    for s in (1, 2, LAST):
        i = rk[s]
        for h in HS:
            if h == 0:
                P.wait_ge(sem("qa", i, 0), len(wide[i]) + len(eng[i]))
            elif s != LAST:
                P.wait_ge(sem("qa", i, 1), len(wide[i]))
            if s == LAST and h == 0:
                P.wait_ge(sem("ex", 0, 0), 2)
            scores(bank[s][h], i, h, 0, 512, s)
    P.wait_ge(S.vq, 1)
    P.wait_ge(S.oq, 1)
    albank = {1: (2, 3), 2: (4, 5), LAST: (6, 7), 0: (0, 1)}
    was = {2: 1, LAST: 2, 0: LAST}
    for s in (1, 2, LAST, 0):
        for h in HS:
            P.wait_ge(sem("qz", s, h if s == LAST else 0), 1)
            if s == 1:
                P.wait_ge(sem("ex", 0, 1), 2)
            else:
                P.wait_ge(sem("ex", was[s], h), 1)
            P.matmul_mx(T["bank%d" % albank[s][h]][:, 0:256], T.pc[:, qsl(s, h)], T.ps[:, qsl(s, h)], T.vc[:], T.vs[:], True, True).then_inc(sem("al", s, h), 1)

    def scored(s, h, n):
        return T["bank%d" % (2 * h + n)][:, 0:256] if s == 0 else T["bank%d" % bank[s][h]][:, 256 * n:256 * n + 256]

    def half_out(q, s, h):
        q.wait_ge(sem("st", s, h), 1)
        q.activation(T.hs[:, 2 * s + h, :], scored(s, h, 0), F.Copy).then_inc(sem("cp", s, h), 1)

    def scan(q, s, h):
        q.wait_ge(sem("st", s, h), 1 if s else 2)
        q.wait_ge(sem("cp", s, h), 1)
        q.tensor_tensor_scan(T.sc[:, 2 * s + h, :], scored(s, h, 1), T.hs[:, 2 * s + h, :], -BIG, O.max, O.max).then_inc(sem("rm", s, h), 1)

    def red(q, s, h):
        q.wait_ge(sem("st", s, h), 1)
        q.tensor_reduce(T.sc[:, 2 * s + h, 255:256], T["bank%d" % bank[s][h]][:], AxisListType.X, O.max).then_inc(sem("rm", s, h), 1)

    def times(q, out, a, f):
        return q.tensor_scalar(out, a, f, None, O.mult) if q is V else q.activation(out, a, F.Copy, scale=f)

    def neg(q, s, h):
        q.wait_ge(sem("rm", s, h), 1)
        col = 2 * rk[s] + h
        times(q, T.nb[:, col:col + 1], T.sc[:, 2 * s + h, 255:256], -A).then_inc(sem("nb", s, h), 1)

    def expo(q, s, h):
        col = 2 * rk[s] + h
        q.wait_ge(sem("nb", s, h), 1)
        for c0, w, src in ((0, 256, scored(0, h, 0)), (256, 256, scored(0, h, 1))) if s == 0 else ((0, 512, T["bank%d" % bank[s][h]][:]),):
            c0 += 512 * h
            q.activation(T["e%d" % s][:, c0:c0 + w], src, F.Exp, bias=T.nb[:, col:col + 1], scale=A).then_inc(sem("ex", s, h), 1)

    def floor0(q, h):
        q.wait_ge(sem("ex", 0, h), 2)
        q.wait_ge(S.ek, 1)
        a = T.e0[:, 512 * h:512 * h + 512]
        q.tensor_scalar(a, a, T.ek[:, 0:1], None, O.max).then_inc(sem("fl", h), 1)

    def turn(q, s, *hs):
        hs = hs or HS
        for h in hs:
            q.wait_ge(sem("ex", s, h) if s else sem("fl", h), 1)
        w = 128 * len(hs)
        for B in range(4):
            c0 = 512 * hs[0]
            d0 = 256 * B + 128 * hs[0] if s == 0 else c0 + w * B
            q.transpose(T["i%d" % s][:, d0:d0 + w], T["e%d" % s][:, c0 + B:c0 + 4 * w:4]).then_inc(sem("tr", s, hs[0] if s else 0), 1)

    def exchange(q, s, h=0, *quads):
        q.wait_ge(sem("tr", s, h), 4 if s else 8)
        for tq in quads or range(4):
            rows = slice(32 * tq, 32 * tq + 32)
            if s == LAST:
                q.dma_start(T["x%d" % s][:, tq, 4 * h:4 * h + 4, :], T["i%d" % s][rows, 512 * h:512 * h + 512]).then_inc(sem("xd", s, h), 16)
            else:
                q.dma_start(T["x%d" % s][:, tq, :, :], T["i%d" % s][rows, :]).then_inc(sem("xd", s, 0), 16)

    def clamp(q, s, h):
        q.wait_ge(sem("xd", s, h if s == LAST else 0), 64)
        if q is V:
            q.wait_ge(S.ek, 1)
        for b in range(4):
            out, src = T["p%d" % s][:, 512 * h + b:512 * h + 512:4], T["x%d" % s][:, :, 4 * h + b, :]
            (q.tensor_scalar(out, src, T.ek[:, 0:1], None, O.max) if q is V else q.activation(out, src, F.Copy)).then_inc(sem("cl", s, h), 1)

    def weave(q, h):
        clamp(q, 0, h)

    def pack(q, s, *hs):
        hs = hs or HS
        for h in hs:
            q.wait_ge(sem("cl", s, h), 4)
        a, b = 128 * hs[0], 128 * hs[-1] + 128
        d = slice(NC * s + a, NC * s + b)
        q.quantize_mx(T.pc[:, d], T.ps[:, d], T["p%d" % s][:, 4 * a:4 * b]).then_inc(sem("qz", s, hs[0]), 1)

    def ekc(q):
        q.wait_ge(S.mk, 1)
        q.activation(T.ek[:, 0:1], T.kc[:, 0:1], F.Exp).then_inc(S.ek, 1)

    def own_c(q):
        for s in range(4):
            for h in HS:
                q.wait_ge(sem("nb", s, h), 1)
        q.activation(T.nbl[:, 8 * r:8 * r + 8], T.nb[:], F.Copy).then_inc(S.cown, 1)
        q.wait_ge(S.mcw, 1)
        q.activation(T.cw[:, 0:8], T.nb[:], F.Copy, scale=-1.0).then_inc(S.cneg, 1)

    def mmax(q):
        q.wait_ge(S.ca, sum(len(eng[i]) for i in others))
        q.wait_ge(S.cown, 1)
        for h in HS:
            q.tensor_reduce(T.mm[:, h:h + 1], T.nbl[:, 2 * r + h:32:8], AxisListType.X, O.min).then_inc(S.mm, 1)

    def wexp(q):
        q.wait_ge(S.mm, 2)
        for h in HS:
            q.activation(T.cw[:, 8 + h:16:2], T.nbl[:, 2 * r + h:32:8], F.Exp, bias=T.mm[:, h:h + 1], scale=-1.0).then_inc(S.wx, 1)
        q.wait_ge(S.wx, 2)

    def turn_cw(q):
        q.wait_ge(S.cneg, 1)
        q.wait_ge(S.wx, 2)
        q.transpose(T.cwt[:], T.cw[:]).then_inc(S.cwt, 1)

    def part(b, n, h):
        return slot(b, n, h, h + 1)

    def wcol(j, h):
        return T.cw[:, 8 + 2 * j + h:9 + 2 * j + h]

    def arrived(q, s, h):
        q.wait_ge(sem("ra", rk[s], h if s == LAST else 0), len(full[rk[s]]))

    def evac(q, s, h):
        q.wait_ge(sem("al", s, h), 1)
        q.activation(part(T.res, s, h), T["bank%d" % albank[s][h]][:, 0:RW], F.Copy).then_inc(sem("ev", s, h), 1)

    def weigh(q, s, h):
        arrived(q, s, h)
        times(q, part(T.tm, s, h), part(T["land"], rk[s], h), wcol(rk[s], h)).then_inc(sem("tm", s, h), 1)

    def own(q, h):
        q.wait_ge(sem("al", 0, h), 1)
        q.wait_ge(S.wx, 2)
        times(q, part(T.acc, 0, h), T["bank%d" % albank[0][h]][:, 0:RW], wcol(r, h)).then_inc(sem("ev", 0, h), 1)

    def add(q, s, h):
        w = 128 if s == LAST else RW
        a = part(T.acc, 0, h)[:, 0:w]
        q.wait_ge(sem("tm", s, h), 1)
        q.wait_ge(sem("ev", 0, h) if s == 1 else sem("ad", s - 1, h), 1)
        q.tensor_tensor(a, a, part(T.tm, s, h)[:, 0:w], O.add).then_inc(sem("ad", s, h), 1)

    def den(q, h):
        q.wait_ge(sem("ad", 2, h), 1)
        arrived(q, LAST, h)
        q.tensor_scalar(T.rd[:, h:h + 1], part(T["land"], diag, h)[:, 128:129], wcol(diag, h), part(T.acc, 0, h)[:, 128:129], O.mult, O.add).then_inc(sem("dn", h), 1)

    def rec(q, h):
        q.wait_ge(sem("dn", h), 1)
        q.reciprocal(T.rd[:, 8 + h:9 + h], T.rd[:, h:h + 1]).then_inc(sem("rc", h), 1)

    def scaled(q, h):
        q.wait_ge(sem("ad", LAST, h), 1)
        q.wait_ge(sem("rc", h), 1)
        times(q, T.on[:, 128 * h:128 * h + 128], part(T.acc, 0, h)[:, 0:128], T.rd[:, 8 + h:9 + h]).then_inc(sem("nr", h), 1)

    def turn_o(q, h):
        q.wait_ge(sem("nr", h), 1)
        q.transpose(T.ot[:, 128 * h:128 * h + 128], T.on[:, 128 * h:128 * h + 128]).then_inc(sem("ott", h), 1)

    def consts(q):
        q.memset(T.one[:], 1.0).then_inc(S.m1, 1)
        q.memset(T.kc[:], -20.0).then_inc(S.mk, 1)
        q.memset(T.cw[:], 0.0).then_inc(S.mcw, 1)
        q.wait_ge(S.m1, 1)
        q.quantize_mx(T.vc[:, 128:256], T.vs[:, 128:256], T.one[:]).then_inc(S.oq, 1)

    def pack_q(q, h):
        q.wait_ge(sem("lq", h), 16)
        q.quantize_mx(T.qc[:, qsl(r, h)], T.qs[:, qsl(r, h)], T.qt[:, 512 * h:512 * h + 512]).then_inc(sem("qq", h), 1)

    def pack_k(q, n):
        q.wait_ge(sem("lk", n), 16)
        q.quantize_mx(T.kcd[:, 256 * n:256 * n + 256], T.ksc[:, 256 * n:256 * n + 256], T.kt[:, 1024 * n:1024 * n + 1024]).then_inc(sem("kq", n), 1)

    def pack_v(q):
        q.wait_ge(S.vp, 4)
        q.quantize_mx(T.vc[:, 0:128], T.vs[:, 0:128], T.vp[:]).then_inc(S.vq, 1)

    def store_p(q, s):
        for h in HS:
            q.wait_ge(sem("cl", s, h), 4)
        q.dma_start(T.p[rk[s]], T["p%d" % s][:]).then_inc(S.stp, 16)

    def wait_ev(q, s, h):
        q.wait_ge(sem("ev", s, h), 1)

    def cw_dram(q):
        q.wait_ge(S.cwt, 1)
        for a in range(4):
            q.dma_start(T.cwd[:, a, :], T.cwt[32 * a:32 * a + 32, :]).then_inc(S.cwd, 16)

    def cw_store(q):
        q.wait_ge(S.cwd, 64)
        q.dma_start(T.c[:, :], T.cwd[0:8, :, :]).then_inc(S.stp, 16)
        q.dma_start(T.w[:, :], T.cwd[8:16, :, :]).then_inc(S.stp, 16)

    CALLS = {"one": consts, "qq": pack_q, "qk": pack_k, "qv": pack_v, "red": red, "scan": scan, "half": half_out, "n": neg, "exp": expo, "floor": floor0,
             "turn": turn, "ex": exchange, "cl": clamp, "weave": weave, "pack": pack, "ek": ekc, "cown": own_c, "mm": mmax, "wexp": wexp,
             "tcw": turn_cw, "ev": evac, "wt": weigh, "own": own, "add": add, "den": den, "rec": rec, "sc": scaled, "to": turn_o, "p": store_p,
             "wev": wait_ev, "cwd": cw_dram, "cw": cw_store}
    for q, order in ((V, VO), (X, XO), (Y, YO)):
        for word in order.split():
            n, *k = word.split(".")
            CALLS[n](q, *[int(x) for x in k])

    def store_o(q, h, quads, sm):
        q.wait_ge(sem("ott", h), 1)
        for tq in quads:
            q.dma_start(T.o[:, 128 * h + 32 * tq:128 * h + 32 * tq + 32], T.ot[32 * tq:32 * tq + 32, 128 * h:128 * h + 128]).then_inc(sm, 16)

    store_o(Y, 0, range(4), S.stp)
    store_o(Y, 1, (0, 1), S.stp)
    store_o(X, 1, (2, 3), S.sto)
    Y.wait_ge(S.stp, 16 * 12)
    X.wait_ge(S.sto, 16 * 2)
